import numpy as np
import ml_dtypes


def mxq(x, axis, fmt="e4m3"):
    dtype, down = {"e4m3": (ml_dtypes.float8_e4m3fn, 7), "e5m2": (ml_dtypes.float8_e5m2, 14)}[fmt]
    v = np.moveaxis(np.asarray(x, np.float32).astype(ml_dtypes.bfloat16).astype(np.float64), axis, -1)
    blocks = v.reshape(v.shape[:-1] + (-1, 32))
    amax = np.abs(blocks).max(-1, keepdims=True)
    byte = np.maximum(np.where(amax > 0, np.frexp(amax)[1] - 1 + 127, 0) - down, 1)
    scale = np.exp2(byte - 127.0)
    codes = (blocks / scale).astype(np.float32).astype(dtype).astype(np.float64)
    return np.moveaxis((codes * scale).reshape(v.shape), -1, axis)


WIDE = False


def mx_kscale(k):
    if not WIDE:
        return np.ones(k)
    levels = np.array([18, -18])
    if k % 512:
        return np.exp2(np.random.permutation(np.resize(levels, k // 32))).repeat(32)
    a = np.empty((k // 512, 16))
    for p in range(k // 512):
        a[p, :8] = np.random.permutation(np.resize(levels, 8))
        for g in range(8):
            far = levels[np.abs(levels - a[p, g]) >= 10]
            a[p, g + 8] = far[np.random.randint(len(far))]
    return np.exp2(a.ravel()).repeat(32)


def f64(x):
    return np.asarray(x).astype(np.float64)


def striped(idx):
    return np.tile(np.asarray(idx).reshape(-1, 16).T, (8, 1)).astype(np.uint16)


def unstriped(offs):
    return offs[:16].T.reshape(-1).astype(np.int64)


E2M1 = np.array([0.0, 0.5, 1.0, 1.5, 2.0, 3.0, 4.0, 6.0, -0.0, -0.5, -1.0, -1.5, -2.0, -3.0, -4.0, -6.0])


def pack_weight(w, fmt):
    k, n = w.shape
    w = f64(np.asarray(w, np.float32).astype(ml_dtypes.bfloat16)).reshape(k // 32, 32, n)
    amax = np.abs(w).max(1)
    if fmt == "e4m3":
        byte = np.frexp(amax)[1] - 1 + 127 - 7
    else:
        mant, ex = np.frexp(amax / 6.0)
        byte = np.where(mant > 0.5, ex, ex - 1) + 127
    byte = np.clip(np.where(amax > 0, byte, 1), 1, 254)
    scaled = (w * np.exp2(127.0 - byte)[:, None, :]).reshape(k, n).astype(np.float32)
    by_word = np.ascontiguousarray(scaled.reshape(k // 512, 128, 4, n).transpose(0, 1, 3, 2))
    if fmt == "e4m3":
        words = by_word.astype(ml_dtypes.float8_e4m3fn).view(np.uint8)
    else:
        c = by_word.astype(ml_dtypes.float4_e2m1fn).view(np.uint8) & 0xF
        words = (c[..., 0::2] | (c[..., 1::2] << 4)).reshape(k // 512, 128, 2 * n)
    return np.ascontiguousarray(words), np.ascontiguousarray(byte.astype(np.uint8).reshape(k // 512, 16, n))


def unpack_weight(words, scales, fmt):
    g, _, n = scales.shape
    words = np.ascontiguousarray(words).reshape(g, 128, n, -1)
    if fmt == "e4m3":
        vals = words.view(ml_dtypes.float8_e4m3fn).astype(np.float64)
    else:
        nib = np.empty((g, 128, n, 4), np.uint8)
        nib[..., 0::2] = words & 0xF
        nib[..., 1::2] = words >> 4
        vals = E2M1[nib]
    vals = vals * np.repeat(np.exp2(scales.astype(np.float64) - 127.0), 8, axis=1)[..., None]
    return vals.transpose(0, 1, 3, 2).reshape(g * 512, n)


def planes(y):
    n, m = y.shape
    v = y.astype(np.float32).astype(ml_dtypes.bfloat16).astype(np.float64).reshape(n // 32, 32, m)
    top = np.abs(v).max(1)
    byte = np.clip(np.where(top > 0, np.frexp(top)[1] - 1 + 127 - 7, 1), 1, 254)
    codes = (v * np.exp2(127.0 - byte)[:, None, :]).reshape(n, m).astype(np.float32).astype(ml_dtypes.float8_e4m3fn).view(np.uint8)
    words = codes.reshape(n // 512, 128, 4, m).transpose(0, 1, 3, 2)
    return np.ascontiguousarray(words), np.ascontiguousarray(byte.astype(np.uint8).reshape(n // 512, 16, m))


def setup_inputs():
    n = np.random.standard_normal
    uni = np.random.uniform
    na = np.random.randint(0, 512, 1024)
    nb = np.random.randint(0, 512, 1024)
    f_m = mx_kscale(512)
    w0_ = pack_weight(n((512, 512)) / np.sqrt(512) / f_m[:, None], "e4m3")
    w1_ = pack_weight(n((512, 512)) / np.sqrt(512) / f_m[:, None], "e4m3")
    w2_ = pack_weight(n((512, 512)) / np.sqrt(512) / f_m[:, None], "e4m3")
    return {
        "dyT": (n((512, 512)) * f_m[:, None]).astype(np.float32),
        "w0_words": w0_[0],
        "w0_scales": w0_[1],
        "w1_words": w1_[0],
        "w1_scales": w1_[1],
        "w2_words": w2_[0],
        "w2_scales": w2_[1],
        "aoffs": striped(na),
        "boffs": striped(nb),
    }


def reference(dyT, w0_words, w0_scales, w1_words, w1_scales, w2_words, w2_scales, aoffs, boffs):
    na = unstriped(aoffs)
    nb = unstriped(boffs)
    w0 = unpack_weight(w0_words, w0_scales, "e4m3")
    w1 = unpack_weight(w1_words, w1_scales, "e4m3")
    w2 = unpack_weight(w2_words, w2_scales, "e4m3")
    q_dyT = mxq(f64(dyT), 0, "e5m2")
    u = w0.T @ q_dyT
    a = w1.T @ q_dyT
    b = w2.T @ q_dyT
    ga = a[:, na]
    sa = ga.reshape(512, 512, 2).sum(-1)
    gb = b[:, nb]
    sb = gb.reshape(512, 512, 2).sum(-1)
    out_0 = u + sa + sb
    return (out_0,) + planes(out_0)

@@ -1,0 +1,142 @@
+from contextlib import ExitStack
+
+import concourse.mybir as mybir
+from concourse.masks import make_identity
+
+F32 = mybir.dt.float32
+BF16 = mybir.dt.bfloat16
+U32 = mybir.dt.uint32
+I32 = mybir.dt.int32
+U16 = mybir.dt.uint16
+U8 = mybir.dt.uint8
+E4M3 = mybir.dt.float8_e4m3fn_x4
+E5M2 = mybir.dt.float8_e5m2_x4
+ADD = mybir.AluOpType.add
+
+P = 128
+LANES = 4
+D = 512
+X = 512
+FAN = 2
+TILES = D // P
+CHUNKS = X // P
+HALF = X // 2
+VECTOR_COLS = 160
+EARLY = (TILES - 1) * P
+
+FLOPS = 3 * 2 * 512 * 512 * 512
+
+
+def tile_attend_grgcn_pl_kernel(tc, dyT, w0_words, w0_scales, w1_words, w1_scales, w2_words, w2_scales,
+                                                 aoffs, boffs, out_0, out_1, out_2):
+    nc = tc.nc
+    with ExitStack() as ctx:
+        lists = ctx.enter_context(tc.tile_pool(name="lists", bufs=1))
+        keep = ctx.enter_context(tc.tile_pool(name="keep", bufs=1))
+        psum = ctx.enter_context(tc.psum_pool(name="psum", bufs=1))
+
+        def load_words(words, name, tag):
+            t = keep.tile([P, D], U32, name=name, tag=tag, align_bytes=64)
+            nc.sync.dma_start(out=t[:].bitcast(I32), in_=words[0].rearrange("p n t -> p (n t)").bitcast(I32))
+            return t
+
+        def load_scales(scales, name, filler, queue):
+            t = keep.tile([P, D], U8, name=name, align_bytes=64)
+            filler.memset(t[:].bitcast(I32), 0)
+            for q in range(4):
+                queue.dma_start(out=t[32 * q:32 * q + 4, :].bitcast(I32), in_=scales[0][4 * q:4 * q + 4, :].bitcast(I32))
+            return t
+
+        dy_rows = dyT.rearrange("(p t) x -> p t x", t=LANES)
+        raw = []
+        for h in range(2):
+            t = keep.tile([P, LANES, HALF], F32, name="raw%d" % h, tag="stage%d" % h, align_bytes=64)
+            nc.sync.dma_start(out=t[:], in_=dy_rows[:, :, h * HALF:(h + 1) * HALF])
+            raw.append(t)
+        w1s = load_scales(w1_scales, "w1s", nc.vector, nc.scalar)
+        w1w = load_words(w1_words, "w1w", "w1w")
+        alist = lists.tile([P, FAN * X // 16], U16, name="alist")
+        nc.sync.dma_start(alist[:], aoffs)
+        blist = lists.tile([P, FAN * X // 16], U16, name="blist")
+        nc.sync.dma_start(blist[:], boffs)
+
+        ident = keep.tile([P, P], F32, name="ident")
+        make_identity(nc, ident[:])
+        w2s = load_scales(w2_scales, "w2s", nc.gpsimd, nc.sync)
+        w0s = load_scales(w0_scales, "w0s", nc.gpsimd, nc.sync)
+
+        dy_codes = keep.tile([P, X], U32, name="dy_codes", align_bytes=64)
+        dy_scales = keep.tile([P, X], U8, name="dy_scales", align_bytes=64)
+        for h in range(2):
+            woven = keep.tile([P, HALF, LANES], BF16, name="woven%d" % h, align_bytes=64)
+            for lo, hi, copy in ((0, VECTOR_COLS, nc.vector.tensor_copy), (VECTOR_COLS, HALF, nc.scalar.copy)):
+                copy(out=woven[:, lo:hi, :].rearrange("p (c i) t -> p c t i", i=4),
+                     in_=raw[h][:, :, lo:hi].rearrange("p t (c i) -> p c t i", i=4))
+            cols = slice(h * HALF, (h + 1) * HALF)
+            nc.vector.quantize_mx(out=dy_codes[:, cols].bitcast(E5M2), scales=dy_scales[:, cols],
+                                  in_=woven[:].rearrange("p x t -> p (x t)"))
+
+        w2w = load_words(w2_words, "w2w", "stage0")
+        w0w = load_words(w0_words, "w0w", "stage1")
+
+        def product(words, scales, name):
+            tiles = []
+            for j in range(TILES):
+                rows = slice(j * P, (j + 1) * P)
+                bank = psum.tile([P, X], F32, name="mm", tag="mm", bufs=3)
+                nc.tensor.matmul_mx(out=bank[:], lhsT=words[:, rows].bitcast(E4M3), lhsT_scale=scales[:, rows],
+                                    rhs=dy_codes[:].bitcast(E5M2), rhs_scale=dy_scales[:], start=True, stop=True)
+                t = keep.tile([P, X], F32, name="%s%d" % (name, j))
+                nc.scalar.copy(out=t[:], in_=bank[:])
+                tiles.append(t)
+            return tiles
+
+        a = product(w1w, w1s, "a")
+        b = product(w2w, w2s, "b")
+        u = product(w0w, w0s, "u")
+
+        y_rows = out_0.rearrange("(p t) x -> p t x", t=LANES)
+        y_words = out_1[0].rearrange("p n t -> p (n t)").bitcast(I32)
+        y_scales = keep.tile([P, X], U8, name="y_scales", align_bytes=64)
+        per = FAN * P // 16
+        for c in range(CHUNKS):
+            cols = slice(c * P, (c + 1) * P)
+            entries = slice(c * per, (c + 1) * per)
+            last = c == CHUNKS - 1
+            ga = []
+            for j in range(TILES):
+                t = keep.tile([P, FAN * P], F32, name="ga", tag="ga", bufs=TILES)
+                nc.vector.tensor_copy(t[:], a[j][:].indirect(alist[:, entries]))
+                ga.append(t)
+            early = psum.tile([P, EARLY], F32, name="early", tag="early", bufs=2)
+            late = psum.tile([P, P], F32, name="late", tag="late", bufs=1)
+            for j in range(TILES):
+                g = keep.tile([P, FAN * P], F32, name="g%d_%d" % (c, j))
+                nc.vector.tensor_tensor(g[:], b[j][:].indirect(blist[:, entries]), ga[j][:], ADD)
+                sums = late[:] if j == TILES - 1 else early[:, j * P:(j + 1) * P]
+                terms = [u[j][:, cols]] + [g[:, k:FAN * P:FAN] for k in range(FAN)]
+                for i, term in enumerate(terms):
+                    nc.tensor.matmul(sums, lhsT=term, rhs=ident[:], is_transpose=True,
+                                     start=(i == 0), stop=(i == len(terms) - 1))
+            dealt = keep.tile([P, LANES, P], F32, name="dealt%d" % c)
+            nc.scalar.copy(out=dealt[:, :, 0:EARLY // LANES], in_=early[:].rearrange("x (p t) -> x t p", t=LANES))
+            nc.scalar.copy(out=dealt[:, :, EARLY // LANES:P], in_=late[:].rearrange("x (p t) -> x t p", t=LANES))
+            back = psum.tile([P, LANES, P], F32, name="back", tag="back", bufs=2)
+            for t in range(LANES):
+                nc.tensor.transpose(back[:, t, :], dealt[:, t, :], ident[:])
+            y = keep.tile([P, LANES, P], F32, name="y%d" % c)
+            nc.scalar.copy(out=y[:], in_=back[:])
+            (nc.scalar if last else nc.sync).dma_start(out=y_rows[:, :, cols], in_=y[:])
+            y_woven = keep.tile([P, P, LANES], BF16, name="y_woven%d" % c, align_bytes=64)
+            if last:
+                nc.vector.tensor_copy(out=y_woven[:].rearrange("p (c i) t -> p c t i", i=4),
+                                      in_=y[:].rearrange("p t (c i) -> p c t i", i=4))
+            else:
+                nc.scalar.copy(out=y_woven[:], in_=back[:].rearrange("p t x -> p x t"))
+            y_codes = keep.tile([P, P], U32, name="y_codes%d" % c, align_bytes=64)
+            nc.vector.quantize_mx(out=y_codes[:].bitcast(E4M3), scales=y_scales[:, cols],
+                                  in_=y_woven[:].rearrange("p x t -> p (x t)"))
+            nc.sync.dma_start(out=y_words[:, cols], in_=y_codes[:].bitcast(I32))
+        for q in range(4):
+            (nc.sync if q % 2 == 0 else nc.scalar).dma_start(out=out_2[0][4 * q:4 * q + 4, :].bitcast(I32),
+                                                             in_=y_scales[32 * q:32 * q + 4, :].bitcast(I32))

@@ -22,7 +22,7 @@ TILES = D // P
 CHUNKS = X // P
 HALF = X // 2
 VECTOR_COLS = 160
-EARLY = (TILES - 1) * P
+PAD = 16
 
 FLOPS = 3 * 2 * 512 * 512 * 512
 
@@ -47,6 +47,8 @@ def tile_attend_grgcn_pl_kernel(tc, dyT, w0_words, w0_scales, w1_words, w1_scale
                 queue.dma_start(out=t[32 * q:32 * q + 4, :].bitcast(I32), in_=scales[0][4 * q:4 * q + 4, :].bitcast(I32))
             return t
 
+        alist = lists.tile([P, FAN * X // 16], U16, name="alist")
+        nc.sync.dma_start(alist[:], aoffs)
         dy_rows = dyT.rearrange("(p t) x -> p t x", t=LANES)
         raw = []
         for h in range(2):
@@ -55,8 +57,6 @@ def tile_attend_grgcn_pl_kernel(tc, dyT, w0_words, w0_scales, w1_words, w1_scale
             raw.append(t)
         w1s = load_scales(w1_scales, "w1s", nc.vector, nc.scalar)
         w1w = load_words(w1_words, "w1w", "w1w")
-        alist = lists.tile([P, FAN * X // 16], U16, name="alist")
-        nc.sync.dma_start(alist[:], aoffs)
         blist = lists.tile([P, FAN * X // 16], U16, name="blist")
         nc.sync.dma_start(blist[:], boffs)
 
@@ -68,7 +68,7 @@ def tile_attend_grgcn_pl_kernel(tc, dyT, w0_words, w0_scales, w1_words, w1_scale
         dy_codes = keep.tile([P, X], U32, name="dy_codes", align_bytes=64)
         dy_scales = keep.tile([P, X], U8, name="dy_scales", align_bytes=64)
         for h in range(2):
-            woven = keep.tile([P, HALF, LANES], BF16, name="woven%d" % h, align_bytes=64)
+            woven = keep.tile([P, HALF, LANES], BF16, name="dy_woven%d" % h, align_bytes=64)
             for lo, hi, copy in ((0, VECTOR_COLS, nc.vector.tensor_copy), (VECTOR_COLS, HALF, nc.scalar.copy)):
                 copy(out=woven[:, lo:hi, :].rearrange("p (c i) t -> p c t i", i=4),
                      in_=raw[h][:, :, lo:hi].rearrange("p t (c i) -> p c t i", i=4))
@@ -79,64 +79,143 @@ def tile_attend_grgcn_pl_kernel(tc, dyT, w0_words, w0_scales, w1_words, w1_scale
         w2w = load_words(w2_words, "w2w", "stage0")
         w0w = load_words(w0_words, "w0w", "stage1")
 
-        def product(words, scales, name):
+        def product(words, scales, name, pad):
             tiles = []
             for j in range(TILES):
                 rows = slice(j * P, (j + 1) * P)
                 bank = psum.tile([P, X], F32, name="mm", tag="mm", bufs=3)
                 nc.tensor.matmul_mx(out=bank[:], lhsT=words[:, rows].bitcast(E4M3), lhsT_scale=scales[:, rows],
                                     rhs=dy_codes[:].bitcast(E5M2), rhs_scale=dy_scales[:], start=True, stop=True)
-                t = keep.tile([P, X], F32, name="%s%d" % (name, j))
-                nc.scalar.copy(out=t[:], in_=bank[:])
+                t = keep.tile([P, X + pad], F32, name="%s%d" % (name, j))
+                if pad:
+                    nc.gpsimd.memset(t[:, X:X + pad], 0.0)
+                nc.scalar.copy(out=t[:, 0:X], in_=bank[:])
                 tiles.append(t)
             return tiles
 
-        a = product(w1w, w1s, "a")
-        b = product(w2w, w2s, "b")
-        u = product(w0w, w0s, "u")
+        a = product(w1w, w1s, "a", PAD)
+        b = product(w2w, w2s, "b", PAD)
+        u = product(w0w, w0s, "u", 0)
 
-        y_rows = out_0.rearrange("(p t) x -> p t x", t=LANES)
+        y_rows = out_0.rearrange("(j p) x -> p j x", p=P)
         y_words = out_1[0].rearrange("p n t -> p (n t)").bitcast(I32)
         y_scales = keep.tile([P, X], U8, name="y_scales", align_bytes=64)
-        per = FAN * P // 16
-        for c in range(CHUNKS):
+
+        y_codes = keep.tile([P, X], U32, name="y_codes", align_bytes=64)
+
+        def gather_first(c):
+            entries = slice(c * FAN * P // 16, (c + 1) * FAN * P // 16)
+            whole = keep.tile([P, TILES * FAN * P], F32, name="first", tag="opening")
+            tiles = [whole[:, j * FAN * P:(j + 1) * FAN * P] for j in range(TILES)]
+            for j in range(TILES):
+                nc.vector.tensor_copy(tiles[j], a[j][:].indirect(alist[:, entries]))
+            return tiles, entries
+
+        def gather_second(out, j, first, entries):
+            nc.vector.tensor_tensor(out, b[j][:].indirect(blist[:, entries]), first[j], ADD)
+
+        def add_turned(sums, c, j, *gathered):
+            terms = [u[j][:, c * P:(c + 1) * P]] + [edges[:, k:FAN * P:FAN] for edges in gathered for k in range(FAN)]
+            for i, term in enumerate(terms):
+                nc.tensor.matmul(sums, lhsT=term, rhs=ident[:], is_transpose=True,
+                                 start=(i == 0), stop=(i == len(terms) - 1))
+
+        def round_out(copy, rounded, sums, lo, hi):
+            copy(out=rounded[:, :, 32 * lo:32 * hi, :], in_=sums[:].rearrange("x (p h e) -> x h p e", h=2, e=2))
+
+        def store_rows(sums, c, lo, hi, tag, queue):
+            n = hi - lo
+            turned = keep.tile([P, n * P], F32, name="turned%d_%d" % (c, lo))
+            nc.scalar.copy(out=turned[:], in_=sums[:])
+            back = psum.tile([P, n, P], F32, name="back", tag=tag, bufs=1)
+            for j in range(n):
+                nc.tensor.transpose(back[:, j, :], turned[:, j * P:(j + 1) * P], ident[:])
+            y = keep.tile([P, n, P], F32, name="y%d_%d" % (c, lo))
+            nc.scalar.copy(out=y[:], in_=back[:])
+            queue.dma_start(out=y_rows[:, lo:hi, c * P:(c + 1) * P], in_=y[:])
+
+        def store_planes(copy, rounded, c, tag):
+            pairs = rounded[:].rearrange("x h p e -> x (h p e)").bitcast(F32)
+            back = psum.tile([P, 2, P], F32, name="pairs_back", tag=tag, bufs=1)
+            for h in range(2):
+                nc.tensor.transpose(back[:, h, :], pairs[:, h * P:(h + 1) * P], ident[:])
+            woven = keep.tile([P, P, LANES], BF16, name="y_woven", tag="woven%d" % c, align_bytes=64)
+            copy(out=woven[:].rearrange("p x t -> p (x t)").bitcast(F32).rearrange("p (x h) -> p x h", h=2),
+                 in_=back[:].rearrange("p h x -> p x h"))
+            quantise(woven, c)
+
+        def quantise(woven, c):
             cols = slice(c * P, (c + 1) * P)
-            entries = slice(c * per, (c + 1) * per)
-            last = c == CHUNKS - 1
-            ga = []
-            for j in range(TILES):
-                t = keep.tile([P, FAN * P], F32, name="ga", tag="ga", bufs=TILES)
-                nc.vector.tensor_copy(t[:], a[j][:].indirect(alist[:, entries]))
-                ga.append(t)
-            early = psum.tile([P, EARLY], F32, name="early", tag="early", bufs=2)
-            late = psum.tile([P, P], F32, name="late", tag="late", bufs=1)
-            for j in range(TILES):
-                g = keep.tile([P, FAN * P], F32, name="g%d_%d" % (c, j))
-                nc.vector.tensor_tensor(g[:], b[j][:].indirect(blist[:, entries]), ga[j][:], ADD)
-                sums = late[:] if j == TILES - 1 else early[:, j * P:(j + 1) * P]
-                terms = [u[j][:, cols]] + [g[:, k:FAN * P:FAN] for k in range(FAN)]
-                for i, term in enumerate(terms):
-                    nc.tensor.matmul(sums, lhsT=term, rhs=ident[:], is_transpose=True,
-                                     start=(i == 0), stop=(i == len(terms) - 1))
+            nc.vector.quantize_mx(out=y_codes[:, cols].bitcast(E4M3), scales=y_scales[:, cols],
+                                  in_=woven[:].rearrange("p x t -> p (x t)"))
+
+        y_lanes = out_0.rearrange("(p t) x -> p t x", t=LANES)
+
+        def finish(sums, c):
+            cols = slice(c * P, (c + 1) * P)
             dealt = keep.tile([P, LANES, P], F32, name="dealt%d" % c)
-            nc.scalar.copy(out=dealt[:, :, 0:EARLY // LANES], in_=early[:].rearrange("x (p t) -> x t p", t=LANES))
-            nc.scalar.copy(out=dealt[:, :, EARLY // LANES:P], in_=late[:].rearrange("x (p t) -> x t p", t=LANES))
-            back = psum.tile([P, LANES, P], F32, name="back", tag="back", bufs=2)
+            nc.scalar.copy(out=dealt[:], in_=sums[:].rearrange("x (p t) -> x t p", t=LANES))
+            back = psum.tile([P, LANES, P], F32, name="back", tag="back", bufs=1)
             for t in range(LANES):
                 nc.tensor.transpose(back[:, t, :], dealt[:, t, :], ident[:])
             y = keep.tile([P, LANES, P], F32, name="y%d" % c)
             nc.scalar.copy(out=y[:], in_=back[:])
-            (nc.scalar if last else nc.sync).dma_start(out=y_rows[:, :, cols], in_=y[:])
-            y_woven = keep.tile([P, P, LANES], BF16, name="y_woven%d" % c, align_bytes=64)
-            if last:
-                nc.vector.tensor_copy(out=y_woven[:].rearrange("p (c i) t -> p c t i", i=4),
-                                      in_=y[:].rearrange("p t (c i) -> p c t i", i=4))
+            nc.sync.dma_start(out=y_lanes[:, :, cols], in_=y[:])
+            woven = keep.tile([P, P, LANES], BF16, name="y_woven", tag="woven%d" % c, align_bytes=64)
+            nc.scalar.copy(out=woven[:], in_=back[:].rearrange("p t x -> p x t"))
+            quantise(woven, c)
+
+        def chunk(c, first, tag):
+            entries = slice(c * FAN * P // 16, (c + 1) * FAN * P // 16)
+            edges = keep.tile([P, TILES * FAN * P], F32, name="edges%d" % c)
+            sums = psum.tile([P, D], F32, name="sums", tag=tag, bufs=1)
+            for j in range(TILES):
+                e = edges[:, j * FAN * P:(j + 1) * FAN * P]
+                nc.vector.tensor_tensor(e, b[j][:].indirect(blist[:, entries]), first[j], ADD)
+                add_turned(sums[:, j * P:(j + 1) * P], c, j, e)
+            finish(sums, c)
+
+        entries = slice(0, 2 * FAN * P // 16)
+        from_a = []
+        for j in range(TILES):
+            t = keep.tile([P, 2 * FAN * P], F32, name="from_a", tag="opening" if j == TILES - 1 else "from_a%d" % j)
+            nc.vector.tensor_copy(t[:], a[j][:].indirect(alist[:, entries]))
+            from_a.append(t)
+        sums = [psum.tile([P, D], F32, name="sums", tag="sums%d" % c, bufs=1) for c in range(2)]
+        for j in range(TILES):
+            t = keep.tile([P, 2 * FAN * P], F32, name="from_b%d" % j)
+            if j == TILES - 1:
+                nc.vector.tensor_tensor(t[:], b[j][:].indirect(blist[:, entries]), from_a[j][:], ADD)
+                parts = [t]
             else:
-                nc.scalar.copy(out=y_woven[:], in_=back[:].rearrange("p t x -> p x t"))
-            y_codes = keep.tile([P, P], U32, name="y_codes%d" % c, align_bytes=64)
-            nc.vector.quantize_mx(out=y_codes[:].bitcast(E4M3), scales=y_scales[:, cols],
-                                  in_=y_woven[:].rearrange("p x t -> p (x t)"))
-            nc.sync.dma_start(out=y_words[:, cols], in_=y_codes[:].bitcast(I32))
+                nc.vector.tensor_copy(t[:], b[j][:].indirect(blist[:, entries]))
+                parts = [from_a[j], t]
+            for c in range(2):
+                add_turned(sums[c][:, j * P:(j + 1) * P], c, j, *[part[:, c * FAN * P:(c + 1) * FAN * P] for part in parts])
+        for c in range(2):
+            finish(sums[c], c)
+        first, entries = gather_first(2)
+        chunk(2, first, "sums1")
+
+        nc.sync.dma_start(out=y_words[:, 0:3 * P], in_=y_codes[:, 0:3 * P].bitcast(I32))
+        late = TILES - 1
+        first, entries = gather_first(3)
+        edges = keep.tile([P, late * FAN * P], F32, name="edges3")
+        early_sums = psum.tile([P, late * P], F32, name="early_sums", tag="sums1", bufs=1)
+        for j in range(late):
+            gather_second(edges[:, j * FAN * P:(j + 1) * FAN * P], j, first, entries)
+            add_turned(early_sums[:, j * P:(j + 1) * P], 3, j, edges[:, j * FAN * P:(j + 1) * FAN * P])
+        late_edges = keep.tile([P, FAN * P], F32, name="late_edges")
+        late_sums = psum.tile([P, P], F32, name="late_sums", tag="back", bufs=1)
+        gather_second(late_edges[:], late, first, entries)
+        add_turned(late_sums[:], 3, late, late_edges[:])
+        rounded = keep.tile([P, 2, P, 2], BF16, name="rounded3")
+        round_out(nc.scalar.copy, rounded, early_sums, 0, late)
+        round_out(nc.vector.tensor_copy, rounded, late_sums, late, TILES)
+        store_planes(nc.vector.tensor_copy, rounded, 3, "sums0")
+        nc.sync.dma_start(out=y_words[:, 3 * P:X], in_=y_codes[:, 3 * P:X].bitcast(I32))
+        store_rows(early_sums, 3, 0, late, "early", nc.sync)
+        store_rows(late_sums, 3, late, TILES, "pairs", nc.scalar)
         for q in range(4):
             (nc.sync if q % 2 == 0 else nc.scalar).dma_start(out=out_2[0][4 * q:4 * q + 4, :].bitcast(I32),
                                                              in_=y_scales[32 * q:32 * q + 4, :].bitcast(I32))

@@ -1,7 +1,6 @@
 from contextlib import ExitStack
 
 import concourse.mybir as mybir
-from concourse.masks import make_identity
 
 F32 = mybir.dt.float32
 BF16 = mybir.dt.bfloat16
@@ -12,210 +11,169 @@ U8 = mybir.dt.uint8
 E4M3 = mybir.dt.float8_e4m3fn_x4
 E5M2 = mybir.dt.float8_e5m2_x4
 ADD = mybir.AluOpType.add
+COPY = mybir.ActivationFunctionType.Copy
 
 P = 128
 LANES = 4
 D = 512
 X = 512
 FAN = 2
-TILES = D // P
-CHUNKS = X // P
 HALF = X // 2
 VECTOR_COLS = 160
 PAD = 16
+QUARTER = X // 4
+VECTOR_FILLS = 2
 
 FLOPS = 3 * 2 * 512 * 512 * 512
 
 
 def tile_attend_grgcn_pl_kernel(tc, dyT, w0_words, w0_scales, w1_words, w1_scales, w2_words, w2_scales,
-                                                 aoffs, boffs, out_0, out_1, out_2):
+                                                     aoffs, boffs, out_0, out_1, out_2):
     nc = tc.nc
     with ExitStack() as ctx:
         lists = ctx.enter_context(tc.tile_pool(name="lists", bufs=1))
         keep = ctx.enter_context(tc.tile_pool(name="keep", bufs=1))
         psum = ctx.enter_context(tc.psum_pool(name="psum", bufs=1))
 
-        def load_words(words, name, tag):
-            t = keep.tile([P, D], U32, name=name, tag=tag, align_bytes=64)
-            nc.sync.dma_start(out=t[:].bitcast(I32), in_=words[0].rearrange("p n t -> p (n t)").bitcast(I32))
+        def load_words(words, name):
+            t = keep.tile([P, D], I32, name=name, align_bytes=64)
+            nc.sync.dma_start(out=t[:], in_=words[0].rearrange("p n t -> p (n t)").bitcast(I32))
             return t
 
-        def load_scales(scales, name, filler, queue):
+        def load_scales(scales, name, queue):
             t = keep.tile([P, D], U8, name=name, align_bytes=64)
-            filler.memset(t[:].bitcast(I32), 0)
             for q in range(4):
-                queue.dma_start(out=t[32 * q:32 * q + 4, :].bitcast(I32), in_=scales[0][4 * q:4 * q + 4, :].bitcast(I32))
+                queue.dma_start(out=t[32 * q:32 * q + 32, :].bitcast(I32),
+                                in_=scales[0][4 * q:4 * q + 4, :].bitcast(I32).partition_broadcast(8))
             return t
 
-        alist = lists.tile([P, FAN * X // 16], U16, name="alist")
-        nc.sync.dma_start(alist[:], aoffs)
+        def deal(words, scales, name, lo, hi):
+            dealt_words = keep.tile([P, hi - lo, P], I32, name="%s_words%d" % (name, lo), align_bytes=64)
+            nc.vector.tensor_copy(out=dealt_words[:].rearrange("k t (c i) -> k c t i", i=4),
+                                  in_=words[:].rearrange("k (c i t) -> k c t i", i=4, t=LANES)[:, :, lo:hi, :])
+            dealt_scales = keep.tile([P, hi - lo, P], U8, name="%s_scales%d" % (name, lo), align_bytes=64)
+            nc.vector.tensor_copy(out=dealt_scales[:].rearrange("k t (c i) -> k c t i", i=16),
+                                  in_=scales[:].rearrange("k (c i t) -> k c t i", i=16, t=LANES)[:, :, lo:hi, :])
+            return [(dealt_words[:, t, :], dealt_scales[:, t, :]) for t in range(hi - lo)]
+
+        def weave(woven, source, lo, hi, copy):
+            copy(out=woven[:, lo:hi, :].rearrange("p (c i) t -> p c t i", i=4),
+                 in_=source[:, :, lo:hi].rearrange("p t (c i) -> p c t i", i=4))
+
         dy_rows = dyT.rearrange("(p t) x -> p t x", t=LANES)
         raw = []
         for h in range(2):
-            t = keep.tile([P, LANES, HALF], F32, name="raw%d" % h, tag="stage%d" % h, align_bytes=64)
+            t = keep.tile([P, LANES, HALF], F32, name="raw%d" % h, align_bytes=64)
             nc.sync.dma_start(out=t[:], in_=dy_rows[:, :, h * HALF:(h + 1) * HALF])
             raw.append(t)
-        w1s = load_scales(w1_scales, "w1s", nc.vector, nc.scalar)
-        w1w = load_words(w1_words, "w1w", "w1w")
+        w1s = load_scales(w1_scales, "w1s", nc.sync)
+        w1w = load_words(w1_words, "w1w")
+        alist = lists.tile([P, FAN * X // 16], U16, name="alist")
+        nc.sync.dma_start(alist[:], aoffs)
+        w2w = load_words(w2_words, "w2w")
+        w2s = load_scales(w2_scales, "w2s", nc.sync)
         blist = lists.tile([P, FAN * X // 16], U16, name="blist")
         nc.sync.dma_start(blist[:], boffs)
+        w0w = load_words(w0_words, "w0w")
+        w0s = load_scales(w0_scales, "w0s", nc.sync)
 
-        ident = keep.tile([P, P], F32, name="ident")
-        make_identity(nc, ident[:])
-        w2s = load_scales(w2_scales, "w2s", nc.gpsimd, nc.sync)
-        w0s = load_scales(w0_scales, "w0s", nc.gpsimd, nc.sync)
+        windows = {}
+        for name in "ab":
+            for t in range(LANES):
+                window = keep.tile([P, X + PAD], F32, name="%s%d" % (name, t))
+                nc.gpsimd.memset(window[:, X:X + PAD], 0.0)
+                windows[name, t] = window
+
 
         dy_codes = keep.tile([P, X], U32, name="dy_codes", align_bytes=64)
         dy_scales = keep.tile([P, X], U8, name="dy_scales", align_bytes=64)
+
+        def product(bank, w, t, cols):
+            nc.tensor.matmul_mx(out=bank[:, cols], lhsT=w[t][0].bitcast(E4M3), lhsT_scale=w[t][1],
+                                rhs=dy_codes[:, cols].bitcast(E5M2), rhs_scale=dy_scales[:, cols], start=True, stop=True)
+
+        a_banks = [psum.tile([P, X], F32, name="a_bank", tag="a_then_u%d" % t) for t in range(LANES)]
         for h in range(2):
             woven = keep.tile([P, HALF, LANES], BF16, name="dy_woven%d" % h, align_bytes=64)
-            for lo, hi, copy in ((0, VECTOR_COLS, nc.vector.tensor_copy), (VECTOR_COLS, HALF, nc.scalar.copy)):
-                copy(out=woven[:, lo:hi, :].rearrange("p (c i) t -> p c t i", i=4),
-                     in_=raw[h][:, :, lo:hi].rearrange("p t (c i) -> p c t i", i=4))
+            weave(woven, raw[h], 0, VECTOR_COLS, nc.vector.tensor_copy)
+            weave(woven, raw[h], VECTOR_COLS, HALF, nc.scalar.copy)
             cols = slice(h * HALF, (h + 1) * HALF)
             nc.vector.quantize_mx(out=dy_codes[:, cols].bitcast(E5M2), scales=dy_scales[:, cols],
                                   in_=woven[:].rearrange("p x t -> p (x t)"))
 
-        w2w = load_words(w2_words, "w2w", "stage0")
-        w0w = load_words(w0_words, "w0w", "stage1")
-
-        def product(words, scales, name, pad):
-            tiles = []
-            for j in range(TILES):
-                rows = slice(j * P, (j + 1) * P)
-                bank = psum.tile([P, X], F32, name="mm", tag="mm", bufs=3)
-                nc.tensor.matmul_mx(out=bank[:], lhsT=words[:, rows].bitcast(E4M3), lhsT_scale=scales[:, rows],
-                                    rhs=dy_codes[:].bitcast(E5M2), rhs_scale=dy_scales[:], start=True, stop=True)
-                t = keep.tile([P, X + pad], F32, name="%s%d" % (name, j))
-                if pad:
-                    nc.gpsimd.memset(t[:, X:X + pad], 0.0)
-                nc.scalar.copy(out=t[:, 0:X], in_=bank[:])
-                tiles.append(t)
-            return tiles
-
-        a = product(w1w, w1s, "a", PAD)
-        b = product(w2w, w2s, "b", PAD)
-        u = product(w0w, w0s, "u", 0)
-
-        y_rows = out_0.rearrange("(j p) x -> p j x", p=P)
-        y_words = out_1[0].rearrange("p n t -> p (n t)").bitcast(I32)
-        y_scales = keep.tile([P, X], U8, name="y_scales", align_bytes=64)
-
+        w1 = deal(w1w, w1s, "w1", 0, 1)
+        w2 = deal(w2w, w2s, "w2", 0, 1)
+        w1 = w1 + deal(w1w, w1s, "w1", 1, LANES)
+        w2 = w2 + deal(w2w, w2s, "w2", 1, LANES)
+        w0 = deal(w0w, w0s, "w0", 0, LANES)
+        every = slice(0, X)
+        y_rows = out_0.rearrange("(p t) x -> p t x", t=LANES)
+        y = keep.tile([P, LANES, X], F32, name="y")
         y_codes = keep.tile([P, X], U32, name="y_codes", align_bytes=64)
+        y_scales = keep.tile([P, X], U8, name="y_scales", align_bytes=64)
+        y_words = out_1[0].rearrange("p n t -> p (n t)").bitcast(I32)
 
-        def gather_first(c):
-            entries = slice(c * FAN * P // 16, (c + 1) * FAN * P // 16)
-            whole = keep.tile([P, TILES * FAN * P], F32, name="first", tag="opening")
-            tiles = [whole[:, j * FAN * P:(j + 1) * FAN * P] for j in range(TILES)]
-            for j in range(TILES):
-                nc.vector.tensor_copy(tiles[j], a[j][:].indirect(alist[:, entries]))
-            return tiles, entries
+        u_banks = {}
+        edges = {}
 
-        def gather_second(out, j, first, entries):
-            nc.vector.tensor_tensor(out, b[j][:].indirect(blist[:, entries]), first[j], ADD)
+        def fill(t):
+            product(a_banks[t], w1, t, every)
+            nc.scalar.copy(out=windows["a", t][:, 0:X], in_=a_banks[t][:])
+            b_bank = psum.tile([P, X], F32, name="b_bank", tag="b%d" % t)
+            product(b_bank, w2, t, every)
+            (nc.vector.tensor_copy if t < VECTOR_FILLS else nc.scalar.copy)(out=windows["b", t][:, 0:X], in_=b_bank[:])
+            u_banks[t] = psum.tile([P, X], F32, name="u_bank", tag="a_then_u%d" % t)
+            product(u_banks[t], w0, t, every)
+            edges[t] = keep.tile([P, X, FAN], F32, name="edges%d" % t)
 
-        def add_turned(sums, c, j, *gathered):
-            terms = [u[j][:, c * P:(c + 1) * P]] + [edges[:, k:FAN * P:FAN] for edges in gathered for k in range(FAN)]
-            for i, term in enumerate(terms):
-                nc.tensor.matmul(sums, lhsT=term, rhs=ident[:], is_transpose=True,
-                                 start=(i == 0), stop=(i == len(terms) - 1))
+        def look_up(t, lo, hi):
+            entries = slice(lo * FAN // 16, hi * FAN // 16)
+            from_a = keep.tile([P, (hi - lo) * FAN], F32, name="from_a%d_%d" % (t, lo))
+            nc.scalar.activation(from_a[:], windows["a", t][:].indirect(alist[:, entries]), COPY)
+            nc.vector.tensor_tensor(edges[t][:, lo:hi, :].rearrange("p x j -> p (x j)"),
+                                    windows["b", t][:].indirect(blist[:, entries]), from_a[:], ADD)
 
-        def round_out(copy, rounded, sums, lo, hi):
-            copy(out=rounded[:, :, 32 * lo:32 * hi, :], in_=sums[:].rearrange("x (p h e) -> x h p e", h=2, e=2))
+        pairs = keep.tile([P, LANES, X], F32, name="pairs")
 
-        def store_rows(sums, c, lo, hi, tag, queue):
-            n = hi - lo
-            turned = keep.tile([P, n * P], F32, name="turned%d_%d" % (c, lo))
-            nc.scalar.copy(out=turned[:], in_=sums[:])
-            back = psum.tile([P, n, P], F32, name="back", tag=tag, bufs=1)
-            for j in range(n):
-                nc.tensor.transpose(back[:, j, :], turned[:, j * P:(j + 1) * P], ident[:])
-            y = keep.tile([P, n, P], F32, name="y%d_%d" % (c, lo))
-            nc.scalar.copy(out=y[:], in_=back[:])
-            queue.dma_start(out=y_rows[:, lo:hi, c * P:(c + 1) * P], in_=y[:])
+        def add_pairs(t, lo, hi):
+            nc.vector.tensor_tensor(pairs[:, t, lo:hi], edges[t][:, lo:hi, 0], edges[t][:, lo:hi, 1], ADD)
 
-        def store_planes(copy, rounded, c, tag):
-            pairs = rounded[:].rearrange("x h p e -> x (h p e)").bitcast(F32)
-            back = psum.tile([P, 2, P], F32, name="pairs_back", tag=tag, bufs=1)
-            for h in range(2):
-                nc.tensor.transpose(back[:, h, :], pairs[:, h * P:(h + 1) * P], ident[:])
-            woven = keep.tile([P, P, LANES], BF16, name="y_woven", tag="woven%d" % c, align_bytes=64)
-            copy(out=woven[:].rearrange("p x t -> p (x t)").bitcast(F32).rearrange("p (x h) -> p x h", h=2),
-                 in_=back[:].rearrange("p h x -> p x h"))
-            quantise(woven, c)
+        def add_self(t, lo, hi):
+            nc.vector.tensor_tensor(y[:, t, lo:hi], u_banks[t][:, lo:hi], pairs[:, t, lo:hi], ADD)
+            nc.sync.dma_start(out=y_rows[:, t, lo:hi], in_=y[:, t, lo:hi])
 
-        def quantise(woven, c):
-            cols = slice(c * P, (c + 1) * P)
-            nc.vector.quantize_mx(out=y_codes[:, cols].bitcast(E4M3), scales=y_scales[:, cols],
-                                  in_=woven[:].rearrange("p x t -> p (x t)"))
+        y_woven = keep.tile([P, X, LANES], BF16, name="y_woven", align_bytes=64)
 
-        y_lanes = out_0.rearrange("(p t) x -> p t x", t=LANES)
+        def planes(lo, hi):
+            nc.vector.quantize_mx(out=y_codes[:, lo:hi].bitcast(E4M3), scales=y_scales[:, lo:hi],
+                                  in_=y_woven[:, lo:hi, :].rearrange("p x t -> p (x t)"))
+            nc.sync.dma_start(out=y_words[:, lo:hi], in_=y_codes[:, lo:hi].bitcast(I32))
 
-        def finish(sums, c):
-            cols = slice(c * P, (c + 1) * P)
-            dealt = keep.tile([P, LANES, P], F32, name="dealt%d" % c)
-            nc.scalar.copy(out=dealt[:], in_=sums[:].rearrange("x (p t) -> x t p", t=LANES))
-            back = psum.tile([P, LANES, P], F32, name="back", tag="back", bufs=1)
-            for t in range(LANES):
-                nc.tensor.transpose(back[:, t, :], dealt[:, t, :], ident[:])
-            y = keep.tile([P, LANES, P], F32, name="y%d" % c)
-            nc.scalar.copy(out=y[:], in_=back[:])
-            nc.sync.dma_start(out=y_lanes[:, :, cols], in_=y[:])
-            woven = keep.tile([P, P, LANES], BF16, name="y_woven", tag="woven%d" % c, align_bytes=64)
-            nc.scalar.copy(out=woven[:], in_=back[:].rearrange("p t x -> p x t"))
-            quantise(woven, c)
-
-        def chunk(c, first, tag):
-            entries = slice(c * FAN * P // 16, (c + 1) * FAN * P // 16)
-            edges = keep.tile([P, TILES * FAN * P], F32, name="edges%d" % c)
-            sums = psum.tile([P, D], F32, name="sums", tag=tag, bufs=1)
-            for j in range(TILES):
-                e = edges[:, j * FAN * P:(j + 1) * FAN * P]
-                nc.vector.tensor_tensor(e, b[j][:].indirect(blist[:, entries]), first[j], ADD)
-                add_turned(sums[:, j * P:(j + 1) * P], c, j, e)
-            finish(sums, c)
-
-        entries = slice(0, 2 * FAN * P // 16)
-        from_a = []
-        for j in range(TILES):
-            t = keep.tile([P, 2 * FAN * P], F32, name="from_a", tag="opening" if j == TILES - 1 else "from_a%d" % j)
-            nc.vector.tensor_copy(t[:], a[j][:].indirect(alist[:, entries]))
-            from_a.append(t)
-        sums = [psum.tile([P, D], F32, name="sums", tag="sums%d" % c, bufs=1) for c in range(2)]
-        for j in range(TILES):
-            t = keep.tile([P, 2 * FAN * P], F32, name="from_b%d" % j)
-            if j == TILES - 1:
-                nc.vector.tensor_tensor(t[:], b[j][:].indirect(blist[:, entries]), from_a[j][:], ADD)
-                parts = [t]
-            else:
-                nc.vector.tensor_copy(t[:], b[j][:].indirect(blist[:, entries]))
-                parts = [from_a[j], t]
-            for c in range(2):
-                add_turned(sums[c][:, j * P:(j + 1) * P], c, j, *[part[:, c * FAN * P:(c + 1) * FAN * P] for part in parts])
-        for c in range(2):
-            finish(sums[c], c)
-        first, entries = gather_first(2)
-        chunk(2, first, "sums1")
-
-        nc.sync.dma_start(out=y_words[:, 0:3 * P], in_=y_codes[:, 0:3 * P].bitcast(I32))
-        late = TILES - 1
-        first, entries = gather_first(3)
-        edges = keep.tile([P, late * FAN * P], F32, name="edges3")
-        early_sums = psum.tile([P, late * P], F32, name="early_sums", tag="sums1", bufs=1)
-        for j in range(late):
-            gather_second(edges[:, j * FAN * P:(j + 1) * FAN * P], j, first, entries)
-            add_turned(early_sums[:, j * P:(j + 1) * P], 3, j, edges[:, j * FAN * P:(j + 1) * FAN * P])
-        late_edges = keep.tile([P, FAN * P], F32, name="late_edges")
-        late_sums = psum.tile([P, P], F32, name="late_sums", tag="back", bufs=1)
-        gather_second(late_edges[:], late, first, entries)
-        add_turned(late_sums[:], 3, late, late_edges[:])
-        rounded = keep.tile([P, 2, P, 2], BF16, name="rounded3")
-        round_out(nc.scalar.copy, rounded, early_sums, 0, late)
-        round_out(nc.vector.tensor_copy, rounded, late_sums, late, TILES)
-        store_planes(nc.vector.tensor_copy, rounded, 3, "sums0")
-        nc.sync.dma_start(out=y_words[:, 3 * P:X], in_=y_codes[:, 3 * P:X].bitcast(I32))
-        store_rows(early_sums, 3, 0, late, "early", nc.sync)
-        store_rows(late_sums, 3, late, TILES, "pairs", nc.scalar)
+        last = LANES - 1
+        for t in range(last):
+            fill(t)
+            look_up(t, 0, HALF)
+            if t > 0:
+                add_pairs(t - 1, 0, X)
+            look_up(t, HALF, X)
+            if t > 0:
+                add_self(t - 1, 0, X)
+        fill(last)
+        look_up(last, 0, HALF)
+        add_pairs(last - 1, 0, X)
+        add_pairs(last, 0, HALF)
+        add_self(last - 1, 0, X)
+        add_self(last, 0, HALF)
+        weave(y_woven, y, 0, HALF, nc.scalar.copy)
+        late = ((HALF, X - QUARTER), (X - QUARTER, X))
+        for step in (look_up, add_pairs, add_self):
+            for lo, hi in late:
+                step(last, lo, hi)
+        planes(0, HALF)
+        weave(y_woven, y, late[0][0], late[0][1], nc.scalar.copy)
+        weave(y_woven, y, late[1][0], late[1][1], nc.vector.tensor_copy)
+        for lo, hi in late:
+            planes(lo, hi)
         for q in range(4):
             (nc.sync if q % 2 == 0 else nc.scalar).dma_start(out=out_2[0][4 * q:4 * q + 4, :].bitcast(I32),
                                                              in_=y_scales[32 * q:32 * q + 4, :].bitcast(I32))

@@ -19,10 +19,9 @@ D = 512
 X = 512
 FAN = 2
 HALF = X // 2
-VECTOR_COLS = 160
 PAD = 16
 QUARTER = X // 4
-VECTOR_FILLS = 2
+PIECES = ((0, HALF), (HALF, X - QUARTER), (X - QUARTER, X))
 
 FLOPS = 3 * 2 * 512 * 512 * 512
 
@@ -41,7 +40,7 @@ def tile_attend_grgcn_pl_kernel(tc, dyT, w0_words, w0_scales, w1_words, w1_scale
             return t
 
         def load_scales(scales, name, queue):
-            t = keep.tile([P, D], U8, name=name, align_bytes=64)
+            t = keep.tile([P, D], U8, name=name, tag=name, align_bytes=64)
             for q in range(4):
                 queue.dma_start(out=t[32 * q:32 * q + 32, :].bitcast(I32),
                                 in_=scales[0][4 * q:4 * q + 4, :].bitcast(I32).partition_broadcast(8))
@@ -61,13 +60,13 @@ def tile_attend_grgcn_pl_kernel(tc, dyT, w0_words, w0_scales, w1_words, w1_scale
                  in_=source[:, :, lo:hi].rearrange("p t (c i) -> p c t i", i=4))
 
         dy_rows = dyT.rearrange("(p t) x -> p t x", t=LANES)
-        raw = []
-        for h in range(2):
-            t = keep.tile([P, LANES, HALF], F32, name="raw%d" % h, align_bytes=64)
-            nc.sync.dma_start(out=t[:], in_=dy_rows[:, :, h * HALF:(h + 1) * HALF])
-            raw.append(t)
-        w1s = load_scales(w1_scales, "w1s", nc.sync)
         w1w = load_words(w1_words, "w1w")
+        w1s = load_scales(w1_scales, "w1s", nc.sync)
+        raw = []
+        for lo, hi in PIECES:
+            t = keep.tile([P, LANES, hi - lo], F32, name="raw%d" % lo, align_bytes=64)
+            nc.sync.dma_start(out=t[:], in_=dy_rows[:, :, lo:hi])
+            raw.append(t)
         alist = lists.tile([P, FAN * X // 16], U16, name="alist")
         nc.sync.dma_start(alist[:], aoffs)
         w2w = load_words(w2_words, "w2w")
@@ -79,33 +78,33 @@ def tile_attend_grgcn_pl_kernel(tc, dyT, w0_words, w0_scales, w1_words, w1_scale
 
         windows = {}
         for name in "ab":
-            for t in range(LANES):
+            for t in range(2):
                 window = keep.tile([P, X + PAD], F32, name="%s%d" % (name, t))
                 nc.gpsimd.memset(window[:, X:X + PAD], 0.0)
                 windows[name, t] = window
+                windows[name, t + 2] = window
 
 
         dy_codes = keep.tile([P, X], U32, name="dy_codes", align_bytes=64)
         dy_scales = keep.tile([P, X], U8, name="dy_scales", align_bytes=64)
 
-        def product(bank, w, t, cols):
-            nc.tensor.matmul_mx(out=bank[:, cols], lhsT=w[t][0].bitcast(E4M3), lhsT_scale=w[t][1],
+        def product(bank, w, t, cols, place=slice(0, X)):
+            nc.tensor.matmul_mx(out=bank[:, place], lhsT=w[t][0].bitcast(E4M3), lhsT_scale=w[t][1],
                                 rhs=dy_codes[:, cols].bitcast(E5M2), rhs_scale=dy_scales[:, cols], start=True, stop=True)
 
-        a_banks = [psum.tile([P, X], F32, name="a_bank", tag="a_then_u%d" % t) for t in range(LANES)]
-        for h in range(2):
-            woven = keep.tile([P, HALF, LANES], BF16, name="dy_woven%d" % h, align_bytes=64)
-            weave(woven, raw[h], 0, VECTOR_COLS, nc.vector.tensor_copy)
-            weave(woven, raw[h], VECTOR_COLS, HALF, nc.scalar.copy)
-            cols = slice(h * HALF, (h + 1) * HALF)
+        w1 = deal(w1w, w1s, "w1", 0, LANES)
+        for (lo, hi), piece in zip(PIECES, raw):
+            woven = keep.tile([P, hi - lo, LANES], BF16, name="dy_woven%d" % lo, align_bytes=64)
+            split = (hi - lo) * 5 // 8
+            weave(woven, piece, 0, split, nc.vector.tensor_copy)
+            weave(woven, piece, split, hi - lo, nc.scalar.copy)
+            cols = slice(lo, hi)
             nc.vector.quantize_mx(out=dy_codes[:, cols].bitcast(E5M2), scales=dy_scales[:, cols],
                                   in_=woven[:].rearrange("p x t -> p (x t)"))
+            part = psum.tile([P, hi - lo], F32, name="part", tag="part%d" % lo)
+            product(part, w1, 0, cols, slice(0, hi - lo))
+            nc.scalar.copy(out=windows["a", 0][:, cols], in_=part[:])
 
-        w1 = deal(w1w, w1s, "w1", 0, 1)
-        w2 = deal(w2w, w2s, "w2", 0, 1)
-        w1 = w1 + deal(w1w, w1s, "w1", 1, LANES)
-        w2 = w2 + deal(w2w, w2s, "w2", 1, LANES)
-        w0 = deal(w0w, w0s, "w0", 0, LANES)
         every = slice(0, X)
         y_rows = out_0.rearrange("(p t) x -> p t x", t=LANES)
         y = keep.tile([P, LANES, X], F32, name="y")
@@ -116,15 +115,18 @@ def tile_attend_grgcn_pl_kernel(tc, dyT, w0_words, w0_scales, w1_words, w1_scale
         u_banks = {}
         edges = {}
 
-        def fill(t):
-            product(a_banks[t], w1, t, every)
-            nc.scalar.copy(out=windows["a", t][:, 0:X], in_=a_banks[t][:])
-            b_bank = psum.tile([P, X], F32, name="b_bank", tag="b%d" % t)
-            product(b_bank, w2, t, every)
-            (nc.vector.tensor_copy if t < VECTOR_FILLS else nc.scalar.copy)(out=windows["b", t][:, 0:X], in_=b_bank[:])
-            u_banks[t] = psum.tile([P, X], F32, name="u_bank", tag="a_then_u%d" % t)
+        def fill(name, w, t, tag, copy):
+            bank = psum.tile([P, X], F32, name="bank", tag=tag)
+            product(bank, w, t, every)
+            copy(out=windows[name, t][:, 0:X], in_=bank[:])
+
+        def self_term(t):
+            u_banks[t] = psum.tile([P, X], F32, name="u_bank", tag="u%d" % t)
             product(u_banks[t], w0, t, every)
-            edges[t] = keep.tile([P, X, FAN], F32, name="edges%d" % t)
+
+        for t in range(LANES):
+            if t != 1:
+                edges[t] = keep.tile([P, X, FAN], F32, name="edges%d" % t)
 
         def look_up(t, lo, hi):
             entries = slice(lo * FAN // 16, hi * FAN // 16)
@@ -150,15 +152,27 @@ def tile_attend_grgcn_pl_kernel(tc, dyT, w0_words, w0_scales, w1_words, w1_scale
             nc.sync.dma_start(out=y_words[:, lo:hi], in_=y_codes[:, lo:hi].bitcast(I32))
 
         last = LANES - 1
-        for t in range(last):
-            fill(t)
+        w2 = deal(w2w, w2s, "w2", 0, 1)
+        b_bank = psum.tile([P, X], F32, name="bank", tag="b0")
+        product(b_bank, w2, 0, every)
+        w2 = w2 + deal(w2w, w2s, "w2", 1, LANES)
+        nc.vector.tensor_copy(out=windows["b", 0][:, 0:X], in_=b_bank[:])
+        look_up(0, 0, QUARTER)
+        look_up(0, QUARTER, HALF)
+        fill("a", w1, 1, "b0", nc.scalar.copy)
+        w0 = deal(w0w, w0s, "w0", 0, LANES)
+        edges[1] = keep.tile([P, X, FAN], F32, name="edges1", tag="w0s", align_bytes=64)
+        for t in range(LANES):
+            self_term(t)
+        fill("b", w2, 1, "part0", nc.vector.tensor_copy)
+        look_up(0, HALF, X)
+        for t in range(1, last):
             look_up(t, 0, HALF)
-            if t > 0:
-                add_pairs(t - 1, 0, X)
+            fill("a", w1, t + 1, "b0", nc.scalar.copy)
+            add_pairs(t - 1, 0, X)
             look_up(t, HALF, X)
-            if t > 0:
-                add_self(t - 1, 0, X)
-        fill(last)
+            fill("b", w2, t + 1, "part0", nc.scalar.copy)
+            add_self(t - 1, 0, X)
         look_up(last, 0, HALF)
         add_pairs(last - 1, 0, X)
         add_pairs(last, 0, HALF)
@@ -166,9 +180,24 @@ def tile_attend_grgcn_pl_kernel(tc, dyT, w0_words, w0_scales, w1_words, w1_scale
         add_self(last, 0, HALF)
         weave(y_woven, y, 0, HALF, nc.scalar.copy)
         late = ((HALF, X - QUARTER), (X - QUARTER, X))
-        for step in (look_up, add_pairs, add_self):
+        found = {}
+        for name, offsets in (("a", alist), ("b", blist)):
             for lo, hi in late:
-                step(last, lo, hi)
+                found[name, lo] = keep.tile([P, hi - lo, FAN], F32, name="late_%s%d" % (name, lo))
+                nc.scalar.activation(found[name, lo][:].rearrange("p x j -> p (x j)"),
+                                     windows[name, last][:].indirect(offsets[:, lo * FAN // 16:hi * FAN // 16]), COPY)
+        sums = {lo: u_banks[last][:, lo:hi] for lo, hi in late}
+        for name in "ab":
+            for j in range(FAN):
+                for lo, hi in late:
+                    if (name, j) == ("b", FAN - 1):
+                        total = y[:, last, lo:hi]
+                    else:
+                        total = keep.tile([P, hi - lo], F32, name="sum_%s%d_%d" % (name, j, lo))[:]
+                    nc.vector.tensor_tensor(total, sums[lo], found[name, lo][:, :, j], ADD)
+                    sums[lo] = total
+        for lo, hi in late:
+            nc.sync.dma_start(out=y_rows[:, last, lo:hi], in_=y[:, last, lo:hi])
         planes(0, HALF)
         weave(y_woven, y, late[0][0], late[0][1], nc.scalar.copy)
         weave(y_woven, y, late[1][0], late[1][1], nc.vector.tensor_copy)

@@ -46,12 +46,12 @@ def tile_attend_grgcn_pl_kernel(tc, dyT, w0_words, w0_scales, w1_words, w1_scale
                                 in_=scales[0][4 * q:4 * q + 4, :].bitcast(I32).partition_broadcast(8))
             return t
 
-        def deal(words, scales, name, lo, hi):
+        def deal(words, scales, name, lo, hi, engine=nc.vector):
             dealt_words = keep.tile([P, hi - lo, P], I32, name="%s_words%d" % (name, lo), align_bytes=64)
-            nc.vector.tensor_copy(out=dealt_words[:].rearrange("k t (c i) -> k c t i", i=4),
+            engine.tensor_copy(out=dealt_words[:].rearrange("k t (c i) -> k c t i", i=4),
                                   in_=words[:].rearrange("k (c i t) -> k c t i", i=4, t=LANES)[:, :, lo:hi, :])
             dealt_scales = keep.tile([P, hi - lo, P], U8, name="%s_scales%d" % (name, lo), align_bytes=64)
-            nc.vector.tensor_copy(out=dealt_scales[:].rearrange("k t (c i) -> k c t i", i=16),
+            engine.tensor_copy(out=dealt_scales[:].rearrange("k t (c i) -> k c t i", i=16),
                                   in_=scales[:].rearrange("k (c i t) -> k c t i", i=16, t=LANES)[:, :, lo:hi, :])
             return [(dealt_words[:, t, :], dealt_scales[:, t, :]) for t in range(hi - lo)]
 
@@ -70,9 +70,9 @@ def tile_attend_grgcn_pl_kernel(tc, dyT, w0_words, w0_scales, w1_words, w1_scale
         alist = lists.tile([P, FAN * X // 16], U16, name="alist")
         nc.sync.dma_start(alist[:], aoffs)
         w2w = load_words(w2_words, "w2w")
-        w2s = load_scales(w2_scales, "w2s", nc.sync)
         blist = lists.tile([P, FAN * X // 16], U16, name="blist")
         nc.sync.dma_start(blist[:], boffs)
+        w2s = load_scales(w2_scales, "w2s", nc.sync)
         w0w = load_words(w0_words, "w0w")
         w0s = load_scales(w0_scales, "w0s", nc.sync)
 
@@ -128,10 +128,11 @@ def tile_attend_grgcn_pl_kernel(tc, dyT, w0_words, w0_scales, w1_words, w1_scale
             if t != 1:
                 edges[t] = keep.tile([P, X, FAN], F32, name="edges%d" % t)
 
-        def look_up(t, lo, hi):
+        def look_up(t, lo, hi, from_a=None):
             entries = slice(lo * FAN // 16, hi * FAN // 16)
-            from_a = keep.tile([P, (hi - lo) * FAN], F32, name="from_a%d_%d" % (t, lo))
-            nc.scalar.activation(from_a[:], windows["a", t][:].indirect(alist[:, entries]), COPY)
+            if from_a is None:
+                from_a = keep.tile([P, (hi - lo) * FAN], F32, name="from_a%d_%d" % (t, lo))
+                nc.scalar.activation(from_a[:], windows["a", t][:].indirect(alist[:, entries]), COPY)
             nc.vector.tensor_tensor(edges[t][:, lo:hi, :].rearrange("p x j -> p (x j)"),
                                     windows["b", t][:].indirect(blist[:, entries]), from_a[:], ADD)
 
@@ -157,52 +158,56 @@ def tile_attend_grgcn_pl_kernel(tc, dyT, w0_words, w0_scales, w1_words, w1_scale
         product(b_bank, w2, 0, every)
         w2 = w2 + deal(w2w, w2s, "w2", 1, LANES)
         nc.vector.tensor_copy(out=windows["b", 0][:, 0:X], in_=b_bank[:])
+        second = keep.tile([P, QUARTER * FAN], F32, name="second", tag="w2s", align_bytes=64)
+        nc.vector.tensor_copy(second[:], windows["a", 0][:].indirect(alist[:, QUARTER * FAN // 16:HALF * FAN // 16]))
         look_up(0, 0, QUARTER)
-        look_up(0, QUARTER, HALF)
+        look_up(0, QUARTER, HALF, second)
+        look_up(0, HALF, X)
         fill("a", w1, 1, "b0", nc.scalar.copy)
-        w0 = deal(w0w, w0s, "w0", 0, LANES)
-        edges[1] = keep.tile([P, X, FAN], F32, name="edges1", tag="w0s", align_bytes=64)
+        w0 = deal(w0w, w0s, "w0", 0, LANES, nc.gpsimd)
+        edges[1] = keep.tile([P, X, FAN], F32, name="edges1")
         for t in range(LANES):
             self_term(t)
         fill("b", w2, 1, "part0", nc.vector.tensor_copy)
-        look_up(0, HALF, X)
         for t in range(1, last):
             look_up(t, 0, HALF)
             fill("a", w1, t + 1, "b0", nc.scalar.copy)
             add_pairs(t - 1, 0, X)
             look_up(t, HALF, X)
-            fill("b", w2, t + 1, "part0", nc.scalar.copy)
+            fill("b", w2, t + 1, ("part384", "part0")[t - 1], nc.scalar.copy)
             add_self(t - 1, 0, X)
-        look_up(last, 0, HALF)
+        look_up(last, 0, QUARTER)
         add_pairs(last - 1, 0, X)
-        add_pairs(last, 0, HALF)
+        add_pairs(last, 0, QUARTER)
         add_self(last - 1, 0, X)
-        add_self(last, 0, HALF)
-        weave(y_woven, y, 0, HALF, nc.scalar.copy)
+        add_self(last, 0, QUARTER)
+
+        def gather(name, offsets, lo, hi):
+            found = keep.tile([P, hi - lo, FAN], F32, name="late_%s%d" % (name, lo))
+            nc.scalar.activation(found[:].rearrange("p x j -> p (x j)"),
+                                 windows[name, last][:].indirect(offsets[:, lo * FAN // 16:hi * FAN // 16]), COPY)
+            return found
+
+        def add_edges(total, start, found, name):
+            first = keep.tile([P, found.shape[1]], F32, name=name)
+            nc.vector.tensor_tensor(first[:], start, found[:, :, 0], ADD)
+            nc.vector.tensor_tensor(total, first[:], found[:, :, 1], ADD)
+
+        with_a = keep.tile([P, X], F32, name="with_a")
+        for lo, hi in ((QUARTER, HALF), (HALF, X)):
+            add_edges(with_a[:, lo:hi], u_banks[last][:, lo:hi], gather("a", alist, lo, hi), "first_a%d" % lo)
+            if lo == QUARTER:
+                add_edges(y[:, last, lo:hi], with_a[:, lo:hi], gather("b", blist, lo, hi), "first_b%d" % lo)
+                nc.sync.dma_start(out=y_rows[:, last, lo:hi], in_=y[:, last, lo:hi])
         late = ((HALF, X - QUARTER), (X - QUARTER, X))
-        found = {}
-        for name, offsets in (("a", alist), ("b", blist)):
-            for lo, hi in late:
-                found[name, lo] = keep.tile([P, hi - lo, FAN], F32, name="late_%s%d" % (name, lo))
-                nc.scalar.activation(found[name, lo][:].rearrange("p x j -> p (x j)"),
-                                     windows[name, last][:].indirect(offsets[:, lo * FAN // 16:hi * FAN // 16]), COPY)
-        sums = {lo: u_banks[last][:, lo:hi] for lo, hi in late}
-        for name in "ab":
-            for j in range(FAN):
-                for lo, hi in late:
-                    if (name, j) == ("b", FAN - 1):
-                        total = y[:, last, lo:hi]
-                    else:
-                        total = keep.tile([P, hi - lo], F32, name="sum_%s%d_%d" % (name, j, lo))[:]
-                    nc.vector.tensor_tensor(total, sums[lo], found[name, lo][:, :, j], ADD)
-                    sums[lo] = total
         for lo, hi in late:
+            add_edges(y[:, last, lo:hi], with_a[:, lo:hi], gather("b", blist, lo, hi), "first_b%d" % lo)
             nc.sync.dma_start(out=y_rows[:, last, lo:hi], in_=y[:, last, lo:hi])
+        weave(y_woven, y, 0, HALF, nc.scalar.copy)
         planes(0, HALF)
-        weave(y_woven, y, late[0][0], late[0][1], nc.scalar.copy)
-        weave(y_woven, y, late[1][0], late[1][1], nc.vector.tensor_copy)
         for lo, hi in late:
-            planes(lo, hi)
+            weave(y_woven, y, lo, hi, nc.vector.tensor_copy)
+        planes(HALF, X)
         for q in range(4):
             (nc.sync if q % 2 == 0 else nc.scalar).dma_start(out=out_2[0][4 * q:4 * q + 4, :].bitcast(I32),
                                                              in_=y_scales[32 * q:32 * q + 4, :].bitcast(I32))

@@ -125,25 +125,36 @@ def tile_attend_grgcn_pl_kernel(tc, dyT, w0_words, w0_scales, w1_words, w1_scale
             product(u_banks[t], w0, t, every)
 
         for t in range(LANES):
-            if t != 1:
-                edges[t] = keep.tile([P, X, FAN], F32, name="edges%d" % t)
+            edges[t] = keep.tile([P, X, FAN], F32, name="edges%d" % t)
 
-        def look_up(t, lo, hi, from_a=None):
-            entries = slice(lo * FAN // 16, hi * FAN // 16)
-            if from_a is None:
-                from_a = keep.tile([P, (hi - lo) * FAN], F32, name="from_a%d_%d" % (t, lo))
-                nc.scalar.activation(from_a[:], windows["a", t][:].indirect(alist[:, entries]), COPY)
+        def gather(name, offsets, t, lo, hi):
+            found = keep.tile([P, hi - lo, FAN], F32, name="found_%s%d_%d" % (name, t, lo))
+            nc.scalar.activation(found[:].rearrange("p x j -> p (x j)"),
+                                 windows[name, t][:].indirect(offsets[:, lo * FAN // 16:hi * FAN // 16]), COPY)
+            return found
+
+        def look_up(t, lo, hi):
+            from_a = gather("a", alist, t, lo, hi)
             nc.vector.tensor_tensor(edges[t][:, lo:hi, :].rearrange("p x j -> p (x j)"),
-                                    windows["b", t][:].indirect(blist[:, entries]), from_a[:], ADD)
+                                    windows["b", t][:].indirect(blist[:, lo * FAN // 16:hi * FAN // 16]),
+                                    from_a[:].rearrange("p x j -> p (x j)"), ADD)
 
-        pairs = keep.tile([P, LANES, X], F32, name="pairs")
+        partial = keep.tile([P, LANES, X], F32, name="partial")
 
-        def add_pairs(t, lo, hi):
-            nc.vector.tensor_tensor(pairs[:, t, lo:hi], edges[t][:, lo:hi, 0], edges[t][:, lo:hi, 1], ADD)
-
-        def add_self(t, lo, hi):
-            nc.vector.tensor_tensor(y[:, t, lo:hi], u_banks[t][:, lo:hi], pairs[:, t, lo:hi], ADD)
+        def store(t, lo, hi):
             nc.sync.dma_start(out=y_rows[:, t, lo:hi], in_=y[:, t, lo:hi])
+
+        def first_add(t, lo, hi):
+            nc.vector.tensor_tensor(partial[:, t, lo:hi], u_banks[t][:, lo:hi], edges[t][:, lo:hi, 0], ADD)
+
+        def second_add(t, lo, hi):
+            (nc.gpsimd if t < 0 else nc.vector).tensor_tensor(y[:, t, lo:hi], partial[:, t, lo:hi], edges[t][:, lo:hi, 1], ADD)
+            store(t, lo, hi)
+
+        def add_edges(total, start, found, name):
+            first = keep.tile([P, found.shape[1]], F32, name=name)
+            nc.vector.tensor_tensor(first[:], start, found[:, :, 0], ADD)
+            nc.vector.tensor_tensor(total, first[:], found[:, :, 1], ADD)
 
         y_woven = keep.tile([P, X, LANES], BF16, name="y_woven", align_bytes=64)
 
@@ -153,60 +164,40 @@ def tile_attend_grgcn_pl_kernel(tc, dyT, w0_words, w0_scales, w1_words, w1_scale
             nc.sync.dma_start(out=y_words[:, lo:hi], in_=y_codes[:, lo:hi].bitcast(I32))
 
         last = LANES - 1
-        w2 = deal(w2w, w2s, "w2", 0, 1)
+        w2 = deal(w2w, w2s, "w2", 0, 1, nc.vector)
         b_bank = psum.tile([P, X], F32, name="bank", tag="b0")
         product(b_bank, w2, 0, every)
-        w2 = w2 + deal(w2w, w2s, "w2", 1, LANES)
+        w2 = w2 + deal(w2w, w2s, "w2", 1, LANES, nc.gpsimd)
         nc.vector.tensor_copy(out=windows["b", 0][:, 0:X], in_=b_bank[:])
-        second = keep.tile([P, QUARTER * FAN], F32, name="second", tag="w2s", align_bytes=64)
-        nc.vector.tensor_copy(second[:], windows["a", 0][:].indirect(alist[:, QUARTER * FAN // 16:HALF * FAN // 16]))
         look_up(0, 0, QUARTER)
-        look_up(0, QUARTER, HALF, second)
-        look_up(0, HALF, X)
+        look_up(0, QUARTER, HALF)
         fill("a", w1, 1, "b0", nc.scalar.copy)
         w0 = deal(w0w, w0s, "w0", 0, LANES, nc.gpsimd)
-        edges[1] = keep.tile([P, X, FAN], F32, name="edges1")
         for t in range(LANES):
             self_term(t)
-        fill("b", w2, 1, "part0", nc.vector.tensor_copy)
+        look_up(0, HALF, X)
+        fill("b", w2, 1, "part0", nc.scalar.copy)
         for t in range(1, last):
             look_up(t, 0, HALF)
             fill("a", w1, t + 1, "b0", nc.scalar.copy)
-            add_pairs(t - 1, 0, X)
+            first_add(t - 1, 0, X)
             look_up(t, HALF, X)
             fill("b", w2, t + 1, ("part384", "part0")[t - 1], nc.scalar.copy)
-            add_self(t - 1, 0, X)
-        look_up(last, 0, QUARTER)
-        add_pairs(last - 1, 0, X)
-        add_pairs(last, 0, QUARTER)
-        add_self(last - 1, 0, X)
-        add_self(last, 0, QUARTER)
-
-        def gather(name, offsets, lo, hi):
-            found = keep.tile([P, hi - lo, FAN], F32, name="late_%s%d" % (name, lo))
-            nc.scalar.activation(found[:].rearrange("p x j -> p (x j)"),
-                                 windows[name, last][:].indirect(offsets[:, lo * FAN // 16:hi * FAN // 16]), COPY)
-            return found
-
-        def add_edges(total, start, found, name):
-            first = keep.tile([P, found.shape[1]], F32, name=name)
-            nc.vector.tensor_tensor(first[:], start, found[:, :, 0], ADD)
-            nc.vector.tensor_tensor(total, first[:], found[:, :, 1], ADD)
-
-        with_a = keep.tile([P, X], F32, name="with_a")
-        for lo, hi in ((QUARTER, HALF), (HALF, X)):
-            add_edges(with_a[:, lo:hi], u_banks[last][:, lo:hi], gather("a", alist, lo, hi), "first_a%d" % lo)
-            if lo == QUARTER:
-                add_edges(y[:, last, lo:hi], with_a[:, lo:hi], gather("b", blist, lo, hi), "first_b%d" % lo)
-                nc.sync.dma_start(out=y_rows[:, last, lo:hi], in_=y[:, last, lo:hi])
+            second_add(t - 1, 0, X)
+        look_up(last, 0, HALF)
+        first_add(last - 1, 0, X)
+        first_add(last, 0, HALF)
+        second_add(last - 1, 0, X)
+        second_add(last, 0, HALF)
+        add_edges(partial[:, last, HALF:X], u_banks[last][:, HALF:X], gather("a", alist, last, HALF, X), "late_a")
         late = ((HALF, X - QUARTER), (X - QUARTER, X))
         for lo, hi in late:
-            add_edges(y[:, last, lo:hi], with_a[:, lo:hi], gather("b", blist, lo, hi), "first_b%d" % lo)
-            nc.sync.dma_start(out=y_rows[:, last, lo:hi], in_=y[:, last, lo:hi])
+            add_edges(y[:, last, lo:hi], partial[:, last, lo:hi], gather("b", blist, last, lo, hi), "late_b%d" % lo)
+            store(last, lo, hi)
         weave(y_woven, y, 0, HALF, nc.scalar.copy)
         planes(0, HALF)
-        for lo, hi in late:
-            weave(y_woven, y, lo, hi, nc.vector.tensor_copy)
+        weave(y_woven, y, late[0][0], late[0][1], nc.scalar.copy)
+        weave(y_woven, y, late[1][0], late[1][1], nc.vector.tensor_copy)
         planes(HALF, X)
         for q in range(4):
             (nc.sync if q % 2 == 0 else nc.scalar).dma_start(out=out_2[0][4 * q:4 * q + 4, :].bitcast(I32),

@@ -133,8 +133,9 @@ def tile_attend_grgcn_pl_kernel(tc, dyT, w0_words, w0_scales, w1_words, w1_scale
                                  windows[name, t][:].indirect(offsets[:, lo * FAN // 16:hi * FAN // 16]), COPY)
             return found
 
-        def look_up(t, lo, hi):
-            from_a = gather("a", alist, t, lo, hi)
+        def look_up(t, lo, hi, from_a=None):
+            if from_a is None:
+                from_a = gather("a", alist, t, lo, hi)
             nc.vector.tensor_tensor(edges[t][:, lo:hi, :].rearrange("p x j -> p (x j)"),
                                     windows["b", t][:].indirect(blist[:, lo * FAN // 16:hi * FAN // 16]),
                                     from_a[:].rearrange("p x j -> p (x j)"), ADD)
@@ -169,14 +170,17 @@ def tile_attend_grgcn_pl_kernel(tc, dyT, w0_words, w0_scales, w1_words, w1_scale
         product(b_bank, w2, 0, every)
         w2 = w2 + deal(w2w, w2s, "w2", 1, LANES, nc.gpsimd)
         nc.vector.tensor_copy(out=windows["b", 0][:, 0:X], in_=b_bank[:])
+        second = keep.tile([P, QUARTER, FAN], F32, name="second", tag="w2s", align_bytes=64)
+        nc.vector.tensor_copy(second[:].rearrange("p x j -> p (x j)"),
+                              windows["a", 0][:].indirect(alist[:, QUARTER * FAN // 16:HALF * FAN // 16]))
         look_up(0, 0, QUARTER)
-        look_up(0, QUARTER, HALF)
+        look_up(0, QUARTER, HALF, second)
+        look_up(0, HALF, X)
         fill("a", w1, 1, "b0", nc.scalar.copy)
         w0 = deal(w0w, w0s, "w0", 0, LANES, nc.gpsimd)
         for t in range(LANES):
             self_term(t)
-        look_up(0, HALF, X)
-        fill("b", w2, 1, "part0", nc.scalar.copy)
+        fill("b", w2, 1, "part0", nc.vector.tensor_copy)
         for t in range(1, last):
             look_up(t, 0, HALF)
             fill("a", w1, t + 1, "b0", nc.scalar.copy)

@@ -15,13 +15,19 @@ COPY = mybir.ActivationFunctionType.Copy
 
 P = 128
 LANES = 4
+LAST = LANES - 1
 D = 512
 X = 512
 FAN = 2
+STRIPE = 16
 HALF = X // 2
-PAD = 16
 QUARTER = X // 4
+PAD = 16
 PIECES = ((0, HALF), (HALF, X - QUARTER), (X - QUARTER, X))
+VECTOR_EIGHTHS = 5
+SLOTS = 6
+EDGE_SLOTS = ((1, 2), (3, 4), (0, 2), (5,))
+PAIR_SLOTS = (0, 5, 1)
 
 FLOPS = 3 * 2 * 512 * 512 * 512
 
@@ -35,46 +41,49 @@ def tile_attend_grgcn_pl_kernel(tc, dyT, w0_words, w0_scales, w1_words, w1_scale
         psum = ctx.enter_context(tc.psum_pool(name="psum", bufs=1))
 
         def load_words(words, name):
-            t = keep.tile([P, D], I32, name=name, align_bytes=64)
-            nc.sync.dma_start(out=t[:], in_=words[0].rearrange("p n t -> p (n t)").bitcast(I32))
-            return t
+            tile = keep.tile([P, D], I32, name=name, align_bytes=64)
+            nc.sync.dma_start(out=tile[:], in_=words[0].rearrange("p n t -> p (n t)").bitcast(I32))
+            return tile
 
-        def load_scales(scales, name, queue):
-            t = keep.tile([P, D], U8, name=name, tag=name, align_bytes=64)
+        def load_scales(scales, name):
+            tile = keep.tile([P, D], U8, name=name, tag=name, align_bytes=64)
             for q in range(4):
-                queue.dma_start(out=t[32 * q:32 * q + 32, :].bitcast(I32),
-                                in_=scales[0][4 * q:4 * q + 4, :].bitcast(I32).partition_broadcast(8))
-            return t
+                nc.sync.dma_start(out=tile[32 * q:32 * q + 32, :].bitcast(I32),
+                                  in_=scales[0][4 * q:4 * q + 4, :].bitcast(I32).partition_broadcast(8))
+            return tile
 
-        def deal(words, scales, name, lo, hi, engine=nc.vector):
-            dealt_words = keep.tile([P, hi - lo, P], I32, name="%s_words%d" % (name, lo), align_bytes=64)
+        def load_list(offsets, name):
+            tile = lists.tile([P, FAN * X // STRIPE], U16, name=name)
+            nc.sync.dma_start(tile[:], offsets)
+            return tile
+
+        def deal(words, scales, name, lo, hi, engine, tag=None):
+            dealt_words = keep.tile([P, hi - lo, P], I32, name="dealt_words", tag=tag or "%s_words%d" % (name, lo), align_bytes=64)
             engine.tensor_copy(out=dealt_words[:].rearrange("k t (c i) -> k c t i", i=4),
-                                  in_=words[:].rearrange("k (c i t) -> k c t i", i=4, t=LANES)[:, :, lo:hi, :])
+                               in_=words[:].rearrange("k (c i t) -> k c t i", i=4, t=LANES)[:, :, lo:hi, :])
             dealt_scales = keep.tile([P, hi - lo, P], U8, name="%s_scales%d" % (name, lo), align_bytes=64)
             engine.tensor_copy(out=dealt_scales[:].rearrange("k t (c i) -> k c t i", i=16),
-                                  in_=scales[:].rearrange("k (c i t) -> k c t i", i=16, t=LANES)[:, :, lo:hi, :])
+                               in_=scales[:].rearrange("k (c i t) -> k c t i", i=16, t=LANES)[:, :, lo:hi, :])
             return [(dealt_words[:, t, :], dealt_scales[:, t, :]) for t in range(hi - lo)]
 
         def weave(woven, source, lo, hi, copy):
             copy(out=woven[:, lo:hi, :].rearrange("p (c i) t -> p c t i", i=4),
                  in_=source[:, :, lo:hi].rearrange("p t (c i) -> p c t i", i=4))
 
+        w1_raw = load_words(w1_words, "w1w")
+        w1_raw_scales = load_scales(w1_scales, "w1s")
         dy_rows = dyT.rearrange("(p t) x -> p t x", t=LANES)
-        w1w = load_words(w1_words, "w1w")
-        w1s = load_scales(w1_scales, "w1s", nc.sync)
-        raw = []
+        dy_pieces = []
         for lo, hi in PIECES:
-            t = keep.tile([P, LANES, hi - lo], F32, name="raw%d" % lo, align_bytes=64)
-            nc.sync.dma_start(out=t[:], in_=dy_rows[:, :, lo:hi])
-            raw.append(t)
-        alist = lists.tile([P, FAN * X // 16], U16, name="alist")
-        nc.sync.dma_start(alist[:], aoffs)
-        w2w = load_words(w2_words, "w2w")
-        blist = lists.tile([P, FAN * X // 16], U16, name="blist")
-        nc.sync.dma_start(blist[:], boffs)
-        w2s = load_scales(w2_scales, "w2s", nc.sync)
-        w0w = load_words(w0_words, "w0w")
-        w0s = load_scales(w0_scales, "w0s", nc.sync)
+            piece = keep.tile([P, LANES, hi - lo], F32, name="raw%d" % lo, align_bytes=64)
+            nc.sync.dma_start(out=piece[:], in_=dy_rows[:, :, lo:hi])
+            dy_pieces.append(piece)
+        lookup = {"a": load_list(aoffs, "alist")}
+        w2_raw = load_words(w2_words, "w2w")
+        lookup["b"] = load_list(boffs, "blist")
+        w2_raw_scales = load_scales(w2_scales, "w2s")
+        w0_raw = load_words(w0_words, "w0w")
+        w0_raw_scales = load_scales(w0_scales, "w0s")
 
         windows = {}
         for name in "ab":
@@ -84,125 +93,138 @@ def tile_attend_grgcn_pl_kernel(tc, dyT, w0_words, w0_scales, w1_words, w1_scale
                 windows[name, t] = window
                 windows[name, t + 2] = window
 
-
         dy_codes = keep.tile([P, X], U32, name="dy_codes", align_bytes=64)
         dy_scales = keep.tile([P, X], U8, name="dy_scales", align_bytes=64)
 
-        def product(bank, w, t, cols, place=slice(0, X)):
-            nc.tensor.matmul_mx(out=bank[:, place], lhsT=w[t][0].bitcast(E4M3), lhsT_scale=w[t][1],
-                                rhs=dy_codes[:, cols].bitcast(E5M2), rhs_scale=dy_scales[:, cols], start=True, stop=True)
+        def product(out, operand, lo, hi):
+            nc.tensor.matmul_mx(out=out, lhsT=operand[0].bitcast(E4M3), lhsT_scale=operand[1],
+                                rhs=dy_codes[:, lo:hi].bitcast(E5M2), rhs_scale=dy_scales[:, lo:hi], start=True, stop=True)
 
-        w1 = deal(w1w, w1s, "w1", 0, LANES)
-        for (lo, hi), piece in zip(PIECES, raw):
+        w1 = deal(w1_raw, w1_raw_scales, "w1", 0, LAST, nc.vector)
+        for (lo, hi), piece in zip(PIECES, dy_pieces):
             woven = keep.tile([P, hi - lo, LANES], BF16, name="dy_woven%d" % lo, align_bytes=64)
-            split = (hi - lo) * 5 // 8
+            split = (hi - lo) * VECTOR_EIGHTHS // 8
             weave(woven, piece, 0, split, nc.vector.tensor_copy)
             weave(woven, piece, split, hi - lo, nc.scalar.copy)
-            cols = slice(lo, hi)
-            nc.vector.quantize_mx(out=dy_codes[:, cols].bitcast(E5M2), scales=dy_scales[:, cols],
+            nc.vector.quantize_mx(out=dy_codes[:, lo:hi].bitcast(E5M2), scales=dy_scales[:, lo:hi],
                                   in_=woven[:].rearrange("p x t -> p (x t)"))
             part = psum.tile([P, hi - lo], F32, name="part", tag="part%d" % lo)
-            product(part, w1, 0, cols, slice(0, hi - lo))
-            nc.scalar.copy(out=windows["a", 0][:, cols], in_=part[:])
+            product(part[:], w1[0], lo, hi)
+            nc.scalar.copy(out=windows["a", 0][:, lo:hi], in_=part[:])
+        first_part, second_part, third_part = ("part%d" % lo for lo, hi in PIECES)
 
-        every = slice(0, X)
         y_rows = out_0.rearrange("(p t) x -> p t x", t=LANES)
         y = keep.tile([P, LANES, X], F32, name="y")
         y_codes = keep.tile([P, X], U32, name="y_codes", align_bytes=64)
         y_scales = keep.tile([P, X], U8, name="y_scales", align_bytes=64)
         y_words = out_1[0].rearrange("p n t -> p (n t)").bitcast(I32)
-
-        u_banks = {}
-        edges = {}
-
-        def fill(name, w, t, tag, copy):
-            bank = psum.tile([P, X], F32, name="bank", tag=tag)
-            product(bank, w, t, every)
-            copy(out=windows[name, t][:, 0:X], in_=bank[:])
-
-        def self_term(t):
-            u_banks[t] = psum.tile([P, X], F32, name="u_bank", tag="u%d" % t)
-            product(u_banks[t], w0, t, every)
-
-        for t in range(LANES):
-            edges[t] = keep.tile([P, X, FAN], F32, name="edges%d" % t)
-
-        def gather(name, offsets, t, lo, hi):
-            found = keep.tile([P, hi - lo, FAN], F32, name="found_%s%d_%d" % (name, t, lo))
-            nc.scalar.activation(found[:].rearrange("p x j -> p (x j)"),
-                                 windows[name, t][:].indirect(offsets[:, lo * FAN // 16:hi * FAN // 16]), COPY)
-            return found
-
-        def look_up(t, lo, hi, from_a=None):
-            if from_a is None:
-                from_a = gather("a", alist, t, lo, hi)
-            nc.vector.tensor_tensor(edges[t][:, lo:hi, :].rearrange("p x j -> p (x j)"),
-                                    windows["b", t][:].indirect(blist[:, lo * FAN // 16:hi * FAN // 16]),
-                                    from_a[:].rearrange("p x j -> p (x j)"), ADD)
-
-        partial = keep.tile([P, LANES, X], F32, name="partial")
-
-        def store(t, lo, hi):
-            nc.sync.dma_start(out=y_rows[:, t, lo:hi], in_=y[:, t, lo:hi])
-
-        def first_add(t, lo, hi):
-            nc.vector.tensor_tensor(partial[:, t, lo:hi], u_banks[t][:, lo:hi], edges[t][:, lo:hi, 0], ADD)
-
-        def second_add(t, lo, hi):
-            (nc.gpsimd if t < 0 else nc.vector).tensor_tensor(y[:, t, lo:hi], partial[:, t, lo:hi], edges[t][:, lo:hi, 1], ADD)
-            store(t, lo, hi)
-
-        def add_edges(total, start, found, name):
-            first = keep.tile([P, found.shape[1]], F32, name=name)
-            nc.vector.tensor_tensor(first[:], start, found[:, :, 0], ADD)
-            nc.vector.tensor_tensor(total, first[:], found[:, :, 1], ADD)
-
+        slots = keep.tile([P, SLOTS, HALF, FAN], F32, name="slots")
+        last_sums = keep.tile([P, X], F32, name="last_sums")
         y_woven = keep.tile([P, X, LANES], BF16, name="y_woven", align_bytes=64)
 
-        def planes(lo, hi):
+        def fill(name, operands, t, bank_tag, copy):
+            bank = psum.tile([P, X], F32, name="bank", tag=bank_tag)
+            product(bank[:], operands[t], 0, X)
+            copy(out=windows[name, t][:, 0:X], in_=bank[:])
+
+        def looked_up(name, t, lo, hi):
+            return windows[name, t][:].indirect(lookup[name][:, lo * FAN // STRIPE:hi * FAN // STRIPE])
+
+        def gather(name, t, lo, hi):
+            found = keep.tile([P, hi - lo, FAN], F32, name="found_%s%d_%d" % (name, t, lo))
+            nc.scalar.activation(found[:].rearrange("p x j -> p (x j)"), looked_up(name, t, lo, hi), COPY)
+            return found
+
+        def gather_b_onto(from_a, t, lo, hi):
+            edges = slots[:, EDGE_SLOTS[t][lo // HALF], lo % HALF:lo % HALF + hi - lo, :]
+            nc.vector.tensor_tensor(edges.rearrange("p x j -> p (x j)"), looked_up("b", t, lo, hi),
+                                    from_a[:].rearrange("p x j -> p (x j)"), ADD)
+
+        def gather_both(t, lo, hi):
+            gather_b_onto(gather("a", t, lo, hi), t, lo, hi)
+
+        def pair_sums(t, lo, hi):
+            if t == LAST:
+                return last_sums[:, lo:hi]
+            return slots[:, PAIR_SLOTS[t], :, :].rearrange("p x j -> p (x j)")[:, lo:hi]
+
+        def add_pairs(t, lo, hi):
+            low, high = EDGE_SLOTS[t][lo // HALF], EDGE_SLOTS[t][(hi - 1) // HALF]
+            width = min(hi - lo, HALF)
+            edges = slots[:, low:high + 1:max(high - low, 1), 0:width, :]
+            nc.vector.tensor_tensor(pair_sums(t, lo, hi).rearrange("p (h x) -> p h x", x=width),
+                                    edges[:, :, :, 0], edges[:, :, :, 1], ADD)
+
+        def add_u(t, lo, hi):
+            nc.vector.tensor_tensor(y[:, t, lo:hi], u[t][:, lo:hi], pair_sums(t, lo, hi), ADD)
+
+        def add_found(total, start, found, name):
+            between = keep.tile([P, found.shape[1]], F32, name=name)
+            nc.vector.tensor_tensor(between[:], start, found[:, :, 0], ADD)
+            nc.vector.tensor_tensor(total, between[:], found[:, :, 1], ADD)
+
+        def store(first_lane, end_lane, lo, hi):
+            nc.sync.dma_start(out=y_rows[:, first_lane:end_lane, lo:hi], in_=y[:, first_lane:end_lane, lo:hi])
+
+        def quantise(lo, hi):
             nc.vector.quantize_mx(out=y_codes[:, lo:hi].bitcast(E4M3), scales=y_scales[:, lo:hi],
                                   in_=y_woven[:, lo:hi, :].rearrange("p x t -> p (x t)"))
             nc.sync.dma_start(out=y_words[:, lo:hi], in_=y_codes[:, lo:hi].bitcast(I32))
 
-        last = LANES - 1
-        w2 = deal(w2w, w2s, "w2", 0, 1, nc.vector)
+        w2 = deal(w2_raw, w2_raw_scales, "w2", 0, 1, nc.vector)
         b_bank = psum.tile([P, X], F32, name="bank", tag="b0")
-        product(b_bank, w2, 0, every)
-        w2 = w2 + deal(w2w, w2s, "w2", 1, LANES, nc.gpsimd)
+        product(b_bank[:], w2[0], 0, X)
+        w2 = w2 + deal(w2_raw, w2_raw_scales, "w2", 1, LANES, nc.gpsimd)
         nc.vector.tensor_copy(out=windows["b", 0][:, 0:X], in_=b_bank[:])
-        second = keep.tile([P, QUARTER, FAN], F32, name="second", tag="w2s", align_bytes=64)
-        nc.vector.tensor_copy(second[:].rearrange("p x j -> p (x j)"),
-                              windows["a", 0][:].indirect(alist[:, QUARTER * FAN // 16:HALF * FAN // 16]))
-        look_up(0, 0, QUARTER)
-        look_up(0, QUARTER, HALF, second)
-        look_up(0, HALF, X)
-        fill("a", w1, 1, "b0", nc.scalar.copy)
-        w0 = deal(w0w, w0s, "w0", 0, LANES, nc.gpsimd)
+        second_quarter = keep.tile([P, QUARTER, FAN], F32, name="second_quarter", tag="w2s", align_bytes=64)
+        nc.vector.tensor_copy(second_quarter[:].rearrange("p x j -> p (x j)"), looked_up("a", 0, QUARTER, HALF))
+        gather_both(0, 0, QUARTER)
+        gather_b_onto(second_quarter, 0, QUARTER, HALF)
+        gather_both(0, HALF, X)
+        fill("a", w1, 1, "a", nc.scalar.copy)
+
+        w0 = deal(w0_raw, w0_raw_scales, "w0", 0, LANES, nc.gpsimd)
+        w1 = w1 + deal(w1_raw, w1_raw_scales, "w1", LAST, LANES, nc.gpsimd, "w0s")
+        u = []
         for t in range(LANES):
-            self_term(t)
-        fill("b", w2, 1, "part0", nc.vector.tensor_copy)
-        for t in range(1, last):
-            look_up(t, 0, HALF)
-            fill("a", w1, t + 1, "b0", nc.scalar.copy)
-            first_add(t - 1, 0, X)
-            look_up(t, HALF, X)
-            fill("b", w2, t + 1, ("part384", "part0")[t - 1], nc.scalar.copy)
-            second_add(t - 1, 0, X)
-        look_up(last, 0, HALF)
-        first_add(last - 1, 0, X)
-        first_add(last, 0, HALF)
-        second_add(last - 1, 0, X)
-        second_add(last, 0, HALF)
-        add_edges(partial[:, last, HALF:X], u_banks[last][:, HALF:X], gather("a", alist, last, HALF, X), "late_a")
-        late = ((HALF, X - QUARTER), (X - QUARTER, X))
-        for lo, hi in late:
-            add_edges(y[:, last, lo:hi], partial[:, last, lo:hi], gather("b", blist, last, lo, hi), "late_b%d" % lo)
-            store(last, lo, hi)
+            u.append(psum.tile([P, X], F32, name="u_bank", tag="u%d" % t if t < LAST else second_part))
+            product(u[t][:], w0[t], 0, X)
+        fill("b", w2, 1, first_part, nc.vector.tensor_copy)
+        add_pairs(0, 0, X)
+
+        for t, a_tag, b_tag, paired in ((1, "b0", third_part, X), (2, "a", first_part, HALF)):
+            gather_both(t, 0, HALF)
+            gather_both(t, HALF, X)
+            fill("a", w1, t + 1, a_tag, nc.scalar.copy)
+            fill("b", w2, t + 1, b_tag, nc.scalar.copy)
+            add_u(t - 1, 0, X)
+            store(t - 1, t, 0, X)
+            add_pairs(t, 0, paired)
+
+        gather_both(LAST, 0, QUARTER)
+        found_a = gather("a", LAST, QUARTER, HALF)
+        found_b = gather("b", LAST, QUARTER, HALF)
+        add_u(LAST - 1, 0, HALF)
+        add_pairs(LAST, 0, QUARTER)
+        add_pairs(LAST - 1, HALF, X)
+        add_u(LAST, 0, QUARTER)
+        add_found(last_sums[:, QUARTER:HALF], u[LAST][:, QUARTER:HALF], found_a, "middle_a")
+        add_found(y[:, LAST, QUARTER:HALF], last_sums[:, QUARTER:HALF], found_b, "middle_b")
+        store(LAST - 1, LANES, 0, HALF)
+        add_found(last_sums[:, HALF:X], u[LAST][:, HALF:X], gather("a", LAST, HALF, X), "late_a")
+        add_u(LAST - 1, HALF, X)
+        store(LAST - 1, LAST, HALF, X)
+        late_quarters = ((HALF, X - QUARTER), (X - QUARTER, X))
+        for lo, hi in late_quarters:
+            add_found(y[:, LAST, lo:hi], last_sums[:, lo:hi], gather("b", LAST, lo, hi), "late_b%d" % lo)
+        store(LAST, LANES, HALF, X)
+
         weave(y_woven, y, 0, HALF, nc.scalar.copy)
-        planes(0, HALF)
-        weave(y_woven, y, late[0][0], late[0][1], nc.scalar.copy)
-        weave(y_woven, y, late[1][0], late[1][1], nc.vector.tensor_copy)
-        planes(HALF, X)
+        quantise(0, HALF)
+        for lo, hi in late_quarters:
+            weave(y_woven, y, lo, hi, nc.vector.tensor_copy)
+        for lo, hi in late_quarters:
+            quantise(lo, hi)
         for q in range(4):
             (nc.sync if q % 2 == 0 else nc.scalar).dma_start(out=out_2[0][4 * q:4 * q + 4, :].bitcast(I32),
                                                              in_=y_scales[32 * q:32 * q + 4, :].bitcast(I32))

@@ -57,12 +57,12 @@ def tile_attend_grgcn_pl_kernel(tc, dyT, w0_words, w0_scales, w1_words, w1_scale
             nc.sync.dma_start(tile[:], offsets)
             return tile
 
-        def deal(words, scales, name, lo, hi, engine, tag=None):
+        def deal(words, scales, name, lo, hi, engine, tag=None, scales_engine=None):
             dealt_words = keep.tile([P, hi - lo, P], I32, name="dealt_words", tag=tag or "%s_words%d" % (name, lo), align_bytes=64)
             engine.tensor_copy(out=dealt_words[:].rearrange("k t (c i) -> k c t i", i=4),
                                in_=words[:].rearrange("k (c i t) -> k c t i", i=4, t=LANES)[:, :, lo:hi, :])
             dealt_scales = keep.tile([P, hi - lo, P], U8, name="%s_scales%d" % (name, lo), align_bytes=64)
-            engine.tensor_copy(out=dealt_scales[:].rearrange("k t (c i) -> k c t i", i=16),
+            (scales_engine or engine).tensor_copy(out=dealt_scales[:].rearrange("k t (c i) -> k c t i", i=16),
                                in_=scales[:].rearrange("k (c i t) -> k c t i", i=16, t=LANES)[:, :, lo:hi, :])
             return [(dealt_words[:, t, :], dealt_scales[:, t, :]) for t in range(hi - lo)]
 
@@ -183,7 +183,7 @@ def tile_attend_grgcn_pl_kernel(tc, dyT, w0_words, w0_scales, w1_words, w1_scale
         gather_both(0, HALF, X)
         fill("a", w1, 1, "a", nc.scalar.copy)
 
-        w0 = deal(w0_raw, w0_raw_scales, "w0", 0, LANES, nc.gpsimd)
+        w0 = deal(w0_raw, w0_raw_scales, "w0", 0, LANES, nc.gpsimd, None, nc.vector)
         w1 = w1 + deal(w1_raw, w1_raw_scales, "w1", LAST, LANES, nc.gpsimd, "w0s")
         u = []
         for t in range(LANES):

@@ -100,7 +100,7 @@ def tile_attend_grgcn_pl_kernel(tc, dyT, w0_words, w0_scales, w1_words, w1_scale
             nc.tensor.matmul_mx(out=out, lhsT=operand[0].bitcast(E4M3), lhsT_scale=operand[1],
                                 rhs=dy_codes[:, lo:hi].bitcast(E5M2), rhs_scale=dy_scales[:, lo:hi], start=True, stop=True)
 
-        w1 = deal(w1_raw, w1_raw_scales, "w1", 0, LAST, nc.vector)
+        w1 = deal(w1_raw, w1_raw_scales, "w1", 0, LANES, nc.vector)
         for (lo, hi), piece in zip(PIECES, dy_pieces):
             woven = keep.tile([P, hi - lo, LANES], BF16, name="dy_woven%d" % lo, align_bytes=64)
             split = (hi - lo) * VECTOR_EIGHTHS // 8
@@ -174,7 +174,7 @@ def tile_attend_grgcn_pl_kernel(tc, dyT, w0_words, w0_scales, w1_words, w1_scale
         w2 = deal(w2_raw, w2_raw_scales, "w2", 0, 1, nc.vector)
         b_bank = psum.tile([P, X], F32, name="bank", tag="b0")
         product(b_bank[:], w2[0], 0, X)
-        w2 = w2 + deal(w2_raw, w2_raw_scales, "w2", 1, LANES, nc.gpsimd)
+        w2 = w2 + deal(w2_raw, w2_raw_scales, "w2", 1, LANES, nc.vector)
         nc.vector.tensor_copy(out=windows["b", 0][:, 0:X], in_=b_bank[:])
         second_quarter = keep.tile([P, QUARTER, FAN], F32, name="second_quarter", tag="w2s", align_bytes=64)
         nc.vector.tensor_copy(second_quarter[:].rearrange("p x j -> p (x j)"), looked_up("a", 0, QUARTER, HALF))
@@ -184,7 +184,6 @@ def tile_attend_grgcn_pl_kernel(tc, dyT, w0_words, w0_scales, w1_words, w1_scale
         fill("a", w1, 1, "a", nc.scalar.copy)
 
         w0 = deal(w0_raw, w0_raw_scales, "w0", 0, LANES, nc.gpsimd, None, nc.vector)
-        w1 = w1 + deal(w1_raw, w1_raw_scales, "w1", LAST, LANES, nc.gpsimd, "w0s")
         u = []
         for t in range(LANES):
             u.append(psum.tile([P, X], F32, name="u_bank", tag="u%d" % t if t < LAST else second_part))
@@ -192,7 +191,7 @@ def tile_attend_grgcn_pl_kernel(tc, dyT, w0_words, w0_scales, w1_words, w1_scale
         fill("b", w2, 1, first_part, nc.vector.tensor_copy)
         add_pairs(0, 0, X)
 
-        for t, a_tag, b_tag, paired in ((1, "b0", third_part, X), (2, "a", first_part, HALF)):
+        for t, a_tag, b_tag, paired in ((1, "b0", third_part, X), (2, third_part, first_part, HALF)):
             gather_both(t, 0, HALF)
             gather_both(t, HALF, X)
             fill("a", w1, t + 1, a_tag, nc.scalar.copy)

@@ -29,6 +29,9 @@ SLOTS = 6
 EDGE_SLOTS = ((1, 2), (3, 4), (0, 2), (5,))
 PAIR_SLOTS = (0, 5, 1)
 
+FOUND = {("a", 0, HALF): "one", ("a", 2, 0): "one", ("a", 1, 0): "two", ("a", 2, HALF): "two",
+         ("a", 1, HALF): "three", ("a", 3, 0): "three"}
+
 FLOPS = 3 * 2 * 512 * 512 * 512
 
 
@@ -57,12 +60,12 @@ def tile_attend_grgcn_pl_kernel(tc, dyT, w0_words, w0_scales, w1_words, w1_scale
             nc.sync.dma_start(tile[:], offsets)
             return tile
 
-        def deal(words, scales, name, lo, hi, engine, tag=None, scales_engine=None):
-            dealt_words = keep.tile([P, hi - lo, P], I32, name="dealt_words", tag=tag or "%s_words%d" % (name, lo), align_bytes=64)
+        def deal(words, scales, name, lo, hi, engine):
+            dealt_words = keep.tile([P, hi - lo, P], I32, name="dealt_words", tag="%s_words%d" % (name, lo), align_bytes=64)
             engine.tensor_copy(out=dealt_words[:].rearrange("k t (c i) -> k c t i", i=4),
                                in_=words[:].rearrange("k (c i t) -> k c t i", i=4, t=LANES)[:, :, lo:hi, :])
             dealt_scales = keep.tile([P, hi - lo, P], U8, name="%s_scales%d" % (name, lo), align_bytes=64)
-            (scales_engine or engine).tensor_copy(out=dealt_scales[:].rearrange("k t (c i) -> k c t i", i=16),
+            engine.tensor_copy(out=dealt_scales[:].rearrange("k t (c i) -> k c t i", i=16),
                                in_=scales[:].rearrange("k (c i t) -> k c t i", i=16, t=LANES)[:, :, lo:hi, :])
             return [(dealt_words[:, t, :], dealt_scales[:, t, :]) for t in range(hi - lo)]
 
@@ -80,10 +83,10 @@ def tile_attend_grgcn_pl_kernel(tc, dyT, w0_words, w0_scales, w1_words, w1_scale
             dy_pieces.append(piece)
         lookup = {"a": load_list(aoffs, "alist")}
         w2_raw = load_words(w2_words, "w2w")
-        lookup["b"] = load_list(boffs, "blist")
         w2_raw_scales = load_scales(w2_scales, "w2s")
         w0_raw = load_words(w0_words, "w0w")
         w0_raw_scales = load_scales(w0_scales, "w0s")
+        lookup["b"] = load_list(boffs, "blist")
 
         windows = {}
         for name in "ab":
@@ -131,7 +134,7 @@ def tile_attend_grgcn_pl_kernel(tc, dyT, w0_words, w0_scales, w1_words, w1_scale
             return windows[name, t][:].indirect(lookup[name][:, lo * FAN // STRIPE:hi * FAN // STRIPE])
 
         def gather(name, t, lo, hi):
-            found = keep.tile([P, hi - lo, FAN], F32, name="found_%s%d_%d" % (name, t, lo))
+            found = keep.tile([P, hi - lo, FAN], F32, name="found", tag=FOUND.get((name, t, lo), "found_%s%d_%d" % (name, t, lo)))
             nc.scalar.activation(found[:].rearrange("p x j -> p (x j)"), looked_up(name, t, lo, hi), COPY)
             return found
 
@@ -183,7 +186,7 @@ def tile_attend_grgcn_pl_kernel(tc, dyT, w0_words, w0_scales, w1_words, w1_scale
         gather_both(0, HALF, X)
         fill("a", w1, 1, "a", nc.scalar.copy)
 
-        w0 = deal(w0_raw, w0_raw_scales, "w0", 0, LANES, nc.gpsimd, None, nc.vector)
+        w0 = deal(w0_raw, w0_raw_scales, "w0", 0, LANES, nc.gpsimd)
         u = []
         for t in range(LANES):
             u.append(psum.tile([P, X], F32, name="u_bank", tag="u%d" % t if t < LAST else second_part))

@@ -89,12 +89,17 @@ def tile_attend_grgcn_pl_kernel(tc, dyT, w0_words, w0_scales, w1_words, w1_scale
         lookup["b"] = load_list(boffs, "blist")
 
         windows = {}
+
+        def open_window(name, t, tag):
+            window = keep.tile([P, X + PAD], F32, name="window", tag=tag, align_bytes=64)
+            nc.gpsimd.memset(window[:, X:X + PAD], 0.0)
+            windows[name, t] = window
+            windows[name, t + 2] = window
+
         for name in "ab":
             for t in range(2):
-                window = keep.tile([P, X + PAD], F32, name="%s%d" % (name, t))
-                nc.gpsimd.memset(window[:, X:X + PAD], 0.0)
-                windows[name, t] = window
-                windows[name, t + 2] = window
+                if (name, t) != ("a", 1):
+                    open_window(name, t, "%s%d" % (name, t))
 
         dy_codes = keep.tile([P, X], U32, name="dy_codes", align_bytes=64)
         dy_scales = keep.tile([P, X], U8, name="dy_scales", align_bytes=64)
@@ -178,13 +183,12 @@ def tile_attend_grgcn_pl_kernel(tc, dyT, w0_words, w0_scales, w1_words, w1_scale
         b_bank = psum.tile([P, X], F32, name="bank", tag="b0")
         product(b_bank[:], w2[0], 0, X)
         w2 = w2 + deal(w2_raw, w2_raw_scales, "w2", 1, LANES, nc.vector)
+        open_window("a", 1, "w2s")
+        fill("a", w1, 1, "a", nc.vector.tensor_copy)
         nc.vector.tensor_copy(out=windows["b", 0][:, 0:X], in_=b_bank[:])
-        second_quarter = keep.tile([P, QUARTER, FAN], F32, name="second_quarter", tag="w2s", align_bytes=64)
-        nc.vector.tensor_copy(second_quarter[:].rearrange("p x j -> p (x j)"), looked_up("a", 0, QUARTER, HALF))
         gather_both(0, 0, QUARTER)
-        gather_b_onto(second_quarter, 0, QUARTER, HALF)
+        gather_both(0, QUARTER, HALF)
         gather_both(0, HALF, X)
-        fill("a", w1, 1, "a", nc.scalar.copy)
 
         w0 = deal(w0_raw, w0_raw_scales, "w0", 0, LANES, nc.gpsimd)
         u = []

@@ -90,9 +90,9 @@ def tile_attend_grgcn_pl_kernel(tc, dyT, w0_words, w0_scales, w1_words, w1_scale
 
         windows = {}
 
-        def open_window(name, t, tag):
+        def open_window(name, t, tag, engine=nc.gpsimd):
             window = keep.tile([P, X + PAD], F32, name="window", tag=tag, align_bytes=64)
-            nc.gpsimd.memset(window[:, X:X + PAD], 0.0)
+            engine.memset(window[:, X:X + PAD], 0.0)
             windows[name, t] = window
             windows[name, t + 2] = window
 
@@ -183,14 +183,18 @@ def tile_attend_grgcn_pl_kernel(tc, dyT, w0_words, w0_scales, w1_words, w1_scale
         b_bank = psum.tile([P, X], F32, name="bank", tag="b0")
         product(b_bank[:], w2[0], 0, X)
         w2 = w2 + deal(w2_raw, w2_raw_scales, "w2", 1, LANES, nc.vector)
-        open_window("a", 1, "w2s")
+        open_window("a", 1, "w2s", nc.vector)
         fill("a", w1, 1, "a", nc.vector.tensor_copy)
         nc.vector.tensor_copy(out=windows["b", 0][:, 0:X], in_=b_bank[:])
         gather_both(0, 0, QUARTER)
         gather_both(0, QUARTER, HALF)
         gather_both(0, HALF, X)
 
-        w0 = deal(w0_raw, w0_raw_scales, "w0", 0, LANES, nc.gpsimd)
+        w0_words_dealt = keep.tile([P, LANES, P], I32, name="w0_words_dealt", align_bytes=64)
+        nc.gpsimd.tensor_copy(out=w0_words_dealt[:], in_=w0_raw[:].rearrange("k (p t) -> k t p", t=LANES))
+        w0_scales_dealt = keep.tile([P, LANES, P], U8, name="w0_scales_dealt", align_bytes=64)
+        nc.gpsimd.tensor_copy(out=w0_scales_dealt[:], in_=w0_raw_scales[:].rearrange("k (p t) -> k t p", t=LANES))
+        w0 = [(w0_words_dealt[:, t, :], w0_scales_dealt[:, t, :]) for t in range(LANES)]
         u = []
         for t in range(LANES):
             u.append(psum.tile([P, X], F32, name="u_bank", tag="u%d" % t if t < LAST else second_part))

@@ -41,15 +41,16 @@ def tile_attend_grgcn_pl_kernel(tc, dyT, w0_words, w0_scales, w1_words, w1_scale
     with ExitStack() as ctx:
         lists = ctx.enter_context(tc.tile_pool(name="lists", bufs=1))
         keep = ctx.enter_context(tc.tile_pool(name="keep", bufs=1))
+        shared = ctx.enter_context(tc.tile_pool(name="shared", bufs=1))
         psum = ctx.enter_context(tc.psum_pool(name="psum", bufs=1))
 
         def load_words(words, name):
-            tile = keep.tile([P, D], I32, name=name, align_bytes=64)
+            tile = keep.tile([P, D], I32, name=name, tag=name, align_bytes=64)
             nc.sync.dma_start(out=tile[:], in_=words[0].rearrange("p n t -> p (n t)").bitcast(I32))
             return tile
 
-        def load_scales(scales, name):
-            tile = keep.tile([P, D], U8, name=name, tag=name, align_bytes=64)
+        def load_scales(scales, name, pool=keep, at=None):
+            tile = pool.tile([P, D], U8, name=name, align_bytes=64, offset=at)
             for q in range(4):
                 nc.sync.dma_start(out=tile[32 * q:32 * q + 32, :].bitcast(I32),
                                   in_=scales[0][4 * q:4 * q + 4, :].bitcast(I32).partition_broadcast(8))
@@ -83,15 +84,15 @@ def tile_attend_grgcn_pl_kernel(tc, dyT, w0_words, w0_scales, w1_words, w1_scale
             dy_pieces.append(piece)
         lookup = {"a": load_list(aoffs, "alist")}
         w2_raw = load_words(w2_words, "w2w")
-        w2_raw_scales = load_scales(w2_scales, "w2s")
+        w2_raw_scales = load_scales(w2_scales, "w2s", shared, 2 * D)
         w0_raw = load_words(w0_words, "w0w")
         w0_raw_scales = load_scales(w0_scales, "w0s")
         lookup["b"] = load_list(boffs, "blist")
 
         windows = {}
 
-        def open_window(name, t, tag, engine=nc.gpsimd):
-            window = keep.tile([P, X + PAD], F32, name="window", tag=tag, align_bytes=64)
+        def open_window(name, t, tag, engine=nc.gpsimd, pool=keep, at=None):
+            window = pool.tile([P, X + PAD], F32, name="window", tag=tag, align_bytes=64, offset=at)
             engine.memset(window[:, X:X + PAD], 0.0)
             windows[name, t] = window
             windows[name, t + 2] = window
@@ -183,11 +184,13 @@ def tile_attend_grgcn_pl_kernel(tc, dyT, w0_words, w0_scales, w1_words, w1_scale
         b_bank = psum.tile([P, X], F32, name="bank", tag="b0")
         product(b_bank[:], w2[0], 0, X)
         w2 = w2 + deal(w2_raw, w2_raw_scales, "w2", 1, LANES, nc.vector)
-        open_window("a", 1, "w2s", nc.vector)
+        open_window("a", 1, "a1", nc.vector, shared, 2 * D + HALF)
         fill("a", w1, 1, "a", nc.vector.tensor_copy)
         nc.vector.tensor_copy(out=windows["b", 0][:, 0:X], in_=b_bank[:])
+        second_quarter = shared.tile([P, QUARTER, FAN], F32, name="second_quarter", align_bytes=64, offset=HALF)
+        nc.vector.tensor_copy(second_quarter[:].rearrange("p x j -> p (x j)"), looked_up("a", 0, QUARTER, HALF))
         gather_both(0, 0, QUARTER)
-        gather_both(0, QUARTER, HALF)
+        gather_b_onto(second_quarter, 0, QUARTER, HALF)
         gather_both(0, HALF, X)
 
         w0_words_dealt = keep.tile([P, LANES, P], I32, name="w0_words_dealt", align_bytes=64)
@@ -211,25 +214,26 @@ def tile_attend_grgcn_pl_kernel(tc, dyT, w0_words, w0_scales, w1_words, w1_scale
             store(t - 1, t, 0, X)
             add_pairs(t, 0, paired)
 
-        gather_both(LAST, 0, QUARTER)
-        found_a = gather("a", LAST, QUARTER, HALF)
-        found_b = gather("b", LAST, QUARTER, HALF)
+        early_a = gather("a", LAST, 0, HALF)
+        early_b = gather("b", LAST, 0, HALF)
+        late_a = gather("a", LAST, HALF, X)
+        late_quarters = ((HALF, X - QUARTER), (X - QUARTER, X))
+        late_b = [gather("b", LAST, lo, hi) for lo, hi in late_quarters]
+        with_first_a = keep.tile([P, HALF], F32, name="with_first_a")
+        nc.vector.tensor_tensor(slots[:, EDGE_SLOTS[LAST][0], :, :], early_a[:], early_b[:], ADD)
         add_u(LAST - 1, 0, HALF)
-        add_pairs(LAST, 0, QUARTER)
+        add_pairs(LAST, 0, HALF)
         add_pairs(LAST - 1, HALF, X)
-        add_u(LAST, 0, QUARTER)
-        add_found(last_sums[:, QUARTER:HALF], u[LAST][:, QUARTER:HALF], found_a, "middle_a")
-        add_found(y[:, LAST, QUARTER:HALF], last_sums[:, QUARTER:HALF], found_b, "middle_b")
+        add_u(LAST, 0, HALF)
         store(LAST - 1, LANES, 0, HALF)
-        add_found(last_sums[:, HALF:X], u[LAST][:, HALF:X], gather("a", LAST, HALF, X), "late_a")
+        weave(y_woven, y, 0, HALF, nc.scalar.copy)
+        nc.vector.tensor_tensor(with_first_a[:], u[LAST][:, HALF:X], late_a[:, :, 0], ADD)
         add_u(LAST - 1, HALF, X)
         store(LAST - 1, LAST, HALF, X)
-        late_quarters = ((HALF, X - QUARTER), (X - QUARTER, X))
-        for lo, hi in late_quarters:
-            add_found(y[:, LAST, lo:hi], last_sums[:, lo:hi], gather("b", LAST, lo, hi), "late_b%d" % lo)
+        nc.vector.tensor_tensor(last_sums[:, HALF:X], with_first_a[:], late_a[:, :, 1], ADD)
+        for (lo, hi), found in zip(late_quarters, late_b):
+            add_found(y[:, LAST, lo:hi], last_sums[:, lo:hi], found, "late_b%d" % lo)
         store(LAST, LANES, HALF, X)
-
-        weave(y_woven, y, 0, HALF, nc.scalar.copy)
         quantise(0, HALF)
         for lo, hi in late_quarters:
             weave(y_woven, y, lo, hi, nc.vector.tensor_copy)

@@ -1,6 +1,7 @@
 from contextlib import ExitStack
 
 import concourse.mybir as mybir
+from concourse.masks import make_identity
 
 F32 = mybir.dt.float32
 BF16 = mybir.dt.bfloat16
@@ -29,8 +30,9 @@ SLOTS = 6
 EDGE_SLOTS = ((1, 2), (3, 4), (0, 2), (5,))
 PAIR_SLOTS = (0, 5, 1)
 
-FOUND = {("a", 0, HALF): "one", ("a", 2, 0): "one", ("a", 1, 0): "two", ("a", 2, HALF): "two",
-         ("a", 1, HALF): "three", ("a", 3, 0): "three"}
+FOUND = {key: "found%d" % (n % 5) for n, key in enumerate((
+    ("a", 0, HALF), ("a", 1, 0), ("a", 1, HALF), ("a", 2, 0), ("a", 2, HALF),
+    ("a", 3, 0), ("b", 3, 0), ("a", 3, HALF), ("b", 3, HALF), ("b", 3, X - QUARTER)))}
 
 FLOPS = 3 * 2 * 512 * 512 * 512
 
@@ -101,6 +103,10 @@ def tile_attend_grgcn_pl_kernel(tc, dyT, w0_words, w0_scales, w1_words, w1_scale
             for t in range(2):
                 if (name, t) != ("a", 1):
                     open_window(name, t, "%s%d" % (name, t))
+        open_window("b", LAST, "b3")
+
+        identity = keep.tile([P, P], F32, name="identity")
+        make_identity(nc, identity[:])
 
         dy_codes = keep.tile([P, X], U32, name="dy_codes", align_bytes=64)
         dy_scales = keep.tile([P, X], U8, name="dy_scales", align_bytes=64)
@@ -128,7 +134,6 @@ def tile_attend_grgcn_pl_kernel(tc, dyT, w0_words, w0_scales, w1_words, w1_scale
         y_scales = keep.tile([P, X], U8, name="y_scales", align_bytes=64)
         y_words = out_1[0].rearrange("p n t -> p (n t)").bitcast(I32)
         slots = keep.tile([P, SLOTS, HALF, FAN], F32, name="slots")
-        last_sums = keep.tile([P, X], F32, name="last_sums")
         y_woven = keep.tile([P, X, LANES], BF16, name="y_woven", align_bytes=64)
 
         def fill(name, operands, t, bank_tag, copy):
@@ -153,8 +158,6 @@ def tile_attend_grgcn_pl_kernel(tc, dyT, w0_words, w0_scales, w1_words, w1_scale
             gather_b_onto(gather("a", t, lo, hi), t, lo, hi)
 
         def pair_sums(t, lo, hi):
-            if t == LAST:
-                return last_sums[:, lo:hi]
             return slots[:, PAIR_SLOTS[t], :, :].rearrange("p x j -> p (x j)")[:, lo:hi]
 
         def add_pairs(t, lo, hi):
@@ -166,11 +169,6 @@ def tile_attend_grgcn_pl_kernel(tc, dyT, w0_words, w0_scales, w1_words, w1_scale
 
         def add_u(t, lo, hi):
             nc.vector.tensor_tensor(y[:, t, lo:hi], u[t][:, lo:hi], pair_sums(t, lo, hi), ADD)
-
-        def add_found(total, start, found, name):
-            between = keep.tile([P, found.shape[1]], F32, name=name)
-            nc.vector.tensor_tensor(between[:], start, found[:, :, 0], ADD)
-            nc.vector.tensor_tensor(total, between[:], found[:, :, 1], ADD)
 
         def store(first_lane, end_lane, lo, hi):
             nc.sync.dma_start(out=y_rows[:, first_lane:end_lane, lo:hi], in_=y[:, first_lane:end_lane, lo:hi])
@@ -205,38 +203,77 @@ def tile_attend_grgcn_pl_kernel(tc, dyT, w0_words, w0_scales, w1_words, w1_scale
         fill("b", w2, 1, first_part, nc.vector.tensor_copy)
         add_pairs(0, 0, X)
 
-        for t, a_tag, b_tag, paired in ((1, "b0", third_part, X), (2, third_part, first_part, HALF)):
-            gather_both(t, 0, HALF)
-            gather_both(t, HALF, X)
-            fill("a", w1, t + 1, a_tag, nc.scalar.copy)
-            fill("b", w2, t + 1, b_tag, nc.scalar.copy)
-            add_u(t - 1, 0, X)
-            store(t - 1, t, 0, X)
-            add_pairs(t, 0, paired)
+        u_last = keep.tile([P, X], F32, name="u_last")
+        turned = keep.tile([P, LANES, P], F32, name="turned")
+        sums = []
 
+        def add_turned(block, found, first, stop):
+            for j in range(FAN):
+                nc.tensor.matmul(sums[block][:], lhsT=found[:, block * P - first:(block + 1) * P - first, j], rhs=identity[:],
+                                 is_transpose=True, start=False, stop=stop and j == FAN - 1)
+
+        def open_with_u(block, tag):
+            sums.append(psum.tile([P, P], F32, name="sums", tag=tag))
+            nc.tensor.matmul(sums[block][:], lhsT=u_last[:, block * P:(block + 1) * P], rhs=identity[:],
+                             is_transpose=True, start=True, stop=False)
+
+        def turn_back(lo, hi, tag, copy):
+            bank = psum.tile([P, hi - lo], F32, name="back", tag=tag)
+            for block in range(lo // P, hi // P):
+                nc.tensor.transpose(bank[:, block * P - lo:(block + 1) * P - lo], turned[:, block, :], identity[:])
+            copy(out=y[:, LAST, lo:hi], in_=bank[:])
+
+        found = gather("a", 1, 0, HALF)
+        fill("a", w1, 2, "b0", nc.scalar.copy)
+        gather_b_onto(found, 1, 0, HALF)
+        fill("b", w2, 2, third_part, nc.vector.tensor_copy)
+        gather_both(1, HALF, X)
+        add_u(0, 0, X)
+        store(0, 1, 0, X)
+        nc.vector.tensor_copy(out=u_last[:], in_=u[LAST][:])
+        add_pairs(1, 0, X)
+
+        gather_both(2, 0, HALF)
+        gather_both(2, HALF, X)
+        fill("a", w1, 3, "a", nc.scalar.copy)
+        fill("b", w2, 3, first_part, nc.scalar.copy)
+        add_u(1, 0, X)
+        store(1, 2, 0, X)
+        add_pairs(2, 0, X)
+
+        for block, tag in enumerate(("a", "b0", "u0", second_part)):
+            open_with_u(block, tag)
         early_a = gather("a", LAST, 0, HALF)
+        for block in (0, 1):
+            add_turned(block, early_a, 0, False)
         early_b = gather("b", LAST, 0, HALF)
+        for block in (0, 1):
+            add_turned(block, early_b, 0, True)
         late_a = gather("a", LAST, HALF, X)
+        for block in (2, 3):
+            add_turned(block, late_a, HALF, False)
+        for block in (0, 1):
+            nc.scalar.copy(out=turned[:, block, :], in_=sums[block][:])
         late_quarters = ((HALF, X - QUARTER), (X - QUARTER, X))
-        late_b = [gather("b", LAST, lo, hi) for lo, hi in late_quarters]
-        with_first_a = keep.tile([P, HALF], F32, name="with_first_a")
-        nc.vector.tensor_tensor(slots[:, EDGE_SLOTS[LAST][0], :, :], early_a[:], early_b[:], ADD)
+        last_found = keep.tile([P, HALF, FAN], F32, name="last_found", tag=FOUND["b", LAST, 0])
+        late_b = [last_found[:, lo - HALF:hi - HALF, :] for lo, hi in late_quarters]
+        for (lo, hi), found in zip(late_quarters, late_b):
+            nc.scalar.activation(found.rearrange("p x j -> p (x j)"), looked_up("b", LAST, lo, hi), COPY)
+        turn_back(0, HALF, third_part, nc.vector.tensor_copy)
         add_u(LAST - 1, 0, HALF)
-        add_pairs(LAST, 0, HALF)
-        add_pairs(LAST - 1, HALF, X)
-        add_u(LAST, 0, HALF)
         store(LAST - 1, LANES, 0, HALF)
-        weave(y_woven, y, 0, HALF, nc.scalar.copy)
-        nc.vector.tensor_tensor(with_first_a[:], u[LAST][:, HALF:X], late_a[:, :, 0], ADD)
         add_u(LAST - 1, HALF, X)
         store(LAST - 1, LAST, HALF, X)
-        nc.vector.tensor_tensor(last_sums[:, HALF:X], with_first_a[:], late_a[:, :, 1], ADD)
-        for (lo, hi), found in zip(late_quarters, late_b):
-            add_found(y[:, LAST, lo:hi], last_sums[:, lo:hi], found, "late_b%d" % lo)
+        for block, found in zip((2, 3), late_b):
+            add_turned(block, found, block * P, True)
+            nc.scalar.copy(out=turned[:, block, :], in_=sums[block][:])
+        for (lo, hi), tag in zip(late_quarters, (first_part, "a")):
+            turn_back(lo, hi, tag, nc.scalar.copy)
         store(LAST, LANES, HALF, X)
+        weave(y_woven, y, 0, HALF, nc.vector.tensor_copy)
+        weave(y_woven, y, HALF, X - QUARTER, nc.vector.tensor_copy)
         quantise(0, HALF)
-        for lo, hi in late_quarters:
-            weave(y_woven, y, lo, hi, nc.vector.tensor_copy)
+        weave(y_woven, y, X - QUARTER, X, nc.vector.tensor_copy)
         for lo, hi in late_quarters:
             quantise(lo, hi)
         for q in range(4):

@@ -260,20 +260,24 @@ def tile_attend_grgcn_pl_kernel(tc, dyT, w0_words, w0_scales, w1_words, w1_scale
         for (lo, hi), found in zip(late_quarters, late_b):
             nc.scalar.activation(found.rearrange("p x j -> p (x j)"), looked_up("b", LAST, lo, hi), COPY)
         turn_back(0, HALF, third_part, nc.vector.tensor_copy)
+        store(LAST, LANES, 0, HALF)
         add_u(LAST - 1, 0, HALF)
-        store(LAST - 1, LANES, 0, HALF)
         add_u(LAST - 1, HALF, X)
-        store(LAST - 1, LAST, HALF, X)
+        store(LAST - 1, LAST, 0, X)
         for block, found in zip((2, 3), late_b):
             add_turned(block, found, block * P, True)
             nc.scalar.copy(out=turned[:, block, :], in_=sums[block][:])
-        for (lo, hi), tag in zip(late_quarters, (first_part, "a")):
-            turn_back(lo, hi, tag, nc.scalar.copy)
+        turn_back(HALF, X - QUARTER, first_part, nc.scalar.copy)
+        nc.scalar.copy(out=y_woven[:, X - QUARTER:X, 0:LAST].rearrange("p (c i) t -> p c t i", i=4),
+                       in_=y[:, 0:LAST, X - QUARTER:X].rearrange("p t (c i) -> p c t i", i=4))
+        last_bank = psum.tile([P, QUARTER], F32, name="last_bank", tag="a")
+        nc.tensor.transpose(last_bank[:], turned[:, LAST, :], identity[:])
+        nc.scalar.copy(out=y_woven[:, X - QUARTER:X, LAST], in_=last_bank[:])
+        nc.scalar.copy(out=y[:, LAST, X - QUARTER:X], in_=last_bank[:])
         store(LAST, LANES, HALF, X)
         weave(y_woven, y, 0, HALF, nc.vector.tensor_copy)
         weave(y_woven, y, HALF, X - QUARTER, nc.vector.tensor_copy)
         quantise(0, HALF)
-        weave(y_woven, y, X - QUARTER, X, nc.vector.tensor_copy)
         for lo, hi in late_quarters:
             quantise(lo, hi)
         for q in range(4):

from contextlib import ExitStack

import concourse.mybir as mybir
from concourse.masks import make_identity

F32 = mybir.dt.float32
BF16 = mybir.dt.bfloat16
U32 = mybir.dt.uint32
I32 = mybir.dt.int32
U16 = mybir.dt.uint16
U8 = mybir.dt.uint8
E4M3 = mybir.dt.float8_e4m3fn_x4
E5M2 = mybir.dt.float8_e5m2_x4
ADD = mybir.AluOpType.add
COPY = mybir.ActivationFunctionType.Copy

P = 128
LANES = 4
LAST = LANES - 1
D = 512
X = 512
FAN = 2
STRIPE = 16
HALF = X // 2
QUARTER = X // 4
PAD = 16
PIECES = ((0, HALF), (HALF, X - QUARTER), (X - QUARTER, X))
VECTOR_EIGHTHS = 5
SLOTS = 6
EDGE_SLOTS = ((1, 2), (3, 4), (0, 2), (5,))
PAIR_SLOTS = (0, 5, 1)

FOUND = {key: "found%d" % (n % 5) for n, key in enumerate((
    ("a", 0, HALF), ("a", 1, 0), ("a", 1, HALF), ("a", 2, 0), ("a", 2, HALF),
    ("a", 3, 0), ("b", 3, 0), ("a", 3, HALF), ("b", 3, HALF), ("b", 3, X - QUARTER)))}

FLOPS = 3 * 2 * 512 * 512 * 512


def tile_attend_grgcn_pl_kernel(tc, dyT, w0_words, w0_scales, w1_words, w1_scales, w2_words, w2_scales,
                                                     aoffs, boffs, out_0, out_1, out_2):
    nc = tc.nc
    with ExitStack() as ctx:
        lists = ctx.enter_context(tc.tile_pool(name="lists", bufs=1))
        keep = ctx.enter_context(tc.tile_pool(name="keep", bufs=1))
        shared = ctx.enter_context(tc.tile_pool(name="shared", bufs=1))
        psum = ctx.enter_context(tc.psum_pool(name="psum", bufs=1))

        def load_words(words, name):
            tile = keep.tile([P, D], I32, name=name, tag=name, align_bytes=64)
            nc.sync.dma_start(out=tile[:], in_=words[0].rearrange("p n t -> p (n t)").bitcast(I32))
            return tile

        def load_scales(scales, name, pool=keep, at=None):
            tile = pool.tile([P, D], U8, name=name, align_bytes=64, offset=at)
            for q in range(4):
                nc.sync.dma_start(out=tile[32 * q:32 * q + 32, :].bitcast(I32),
                                  in_=scales[0][4 * q:4 * q + 4, :].bitcast(I32).partition_broadcast(8))
            return tile

        def load_list(offsets, name):
            tile = lists.tile([P, FAN * X // STRIPE], U16, name=name)
            nc.sync.dma_start(tile[:], offsets)
            return tile

        def deal(words, scales, name, lo, hi, engine):
            dealt_words = keep.tile([P, hi - lo, P], I32, name="dealt_words", tag="%s_words%d" % (name, lo), align_bytes=64)
            engine.tensor_copy(out=dealt_words[:].rearrange("k t (c i) -> k c t i", i=4),
                               in_=words[:].rearrange("k (c i t) -> k c t i", i=4, t=LANES)[:, :, lo:hi, :])
            dealt_scales = keep.tile([P, hi - lo, P], U8, name="%s_scales%d" % (name, lo), align_bytes=64)
            engine.tensor_copy(out=dealt_scales[:].rearrange("k t (c i) -> k c t i", i=16),
                               in_=scales[:].rearrange("k (c i t) -> k c t i", i=16, t=LANES)[:, :, lo:hi, :])
            return [(dealt_words[:, t, :], dealt_scales[:, t, :]) for t in range(hi - lo)]

        def weave(woven, source, lo, hi, copy):
            copy(out=woven[:, lo:hi, :].rearrange("p (c i) t -> p c t i", i=4),
                 in_=source[:, :, lo:hi].rearrange("p t (c i) -> p c t i", i=4))

        w1_raw = load_words(w1_words, "w1w")
        w1_raw_scales = load_scales(w1_scales, "w1s")
        dy_rows = dyT.rearrange("(p t) x -> p t x", t=LANES)
        dy_pieces = []
        for lo, hi in PIECES:
            piece = keep.tile([P, LANES, hi - lo], F32, name="raw%d" % lo, align_bytes=64)
            nc.sync.dma_start(out=piece[:], in_=dy_rows[:, :, lo:hi])
            dy_pieces.append(piece)
        lookup = {"a": load_list(aoffs, "alist")}
        w2_raw = load_words(w2_words, "w2w")
        w2_raw_scales = load_scales(w2_scales, "w2s", shared, 2 * D)
        w0_raw = load_words(w0_words, "w0w")
        w0_raw_scales = load_scales(w0_scales, "w0s")
        lookup["b"] = load_list(boffs, "blist")

        windows = {}

        def open_window(name, t, tag, engine=nc.gpsimd, pool=keep, at=None):
            window = pool.tile([P, X + PAD], F32, name="window", tag=tag, align_bytes=64, offset=at)
            engine.memset(window[:, X:X + PAD], 0.0)
            windows[name, t] = window
            windows[name, t + 2] = window

        for name in "ab":
            for t in range(2):
                if (name, t) != ("a", 1):
                    open_window(name, t, "%s%d" % (name, t))
        open_window("b", LAST, "b3")

        identity = keep.tile([P, P], F32, name="identity")
        make_identity(nc, identity[:])

        dy_codes = keep.tile([P, X], U32, name="dy_codes", align_bytes=64)
        dy_scales = keep.tile([P, X], U8, name="dy_scales", align_bytes=64)

        def product(out, operand, lo, hi):
            nc.tensor.matmul_mx(out=out, lhsT=operand[0].bitcast(E4M3), lhsT_scale=operand[1],
                                rhs=dy_codes[:, lo:hi].bitcast(E5M2), rhs_scale=dy_scales[:, lo:hi], start=True, stop=True)

        w1 = deal(w1_raw, w1_raw_scales, "w1", 0, LANES, nc.vector)
        for (lo, hi), piece in zip(PIECES, dy_pieces):
            woven = keep.tile([P, hi - lo, LANES], BF16, name="dy_woven%d" % lo, align_bytes=64)
            split = (hi - lo) * VECTOR_EIGHTHS // 8
            weave(woven, piece, 0, split, nc.vector.tensor_copy)
            weave(woven, piece, split, hi - lo, nc.scalar.copy)
            nc.vector.quantize_mx(out=dy_codes[:, lo:hi].bitcast(E5M2), scales=dy_scales[:, lo:hi],
                                  in_=woven[:].rearrange("p x t -> p (x t)"))
            part = psum.tile([P, hi - lo], F32, name="part", tag="part%d" % lo)
            product(part[:], w1[0], lo, hi)
            nc.scalar.copy(out=windows["a", 0][:, lo:hi], in_=part[:])
        first_part, second_part, third_part = ("part%d" % lo for lo, hi in PIECES)

        y_rows = out_0.rearrange("(p t) x -> p t x", t=LANES)
        y = keep.tile([P, LANES, X], F32, name="y")
        y_codes = keep.tile([P, X], U32, name="y_codes", align_bytes=64)
        y_scales = keep.tile([P, X], U8, name="y_scales", align_bytes=64)
        y_words = out_1[0].rearrange("p n t -> p (n t)").bitcast(I32)
        slots = keep.tile([P, SLOTS, HALF, FAN], F32, name="slots")
        y_woven = keep.tile([P, X, LANES], BF16, name="y_woven", align_bytes=64)

        def fill(name, operands, t, bank_tag, copy):
            bank = psum.tile([P, X], F32, name="bank", tag=bank_tag)
            product(bank[:], operands[t], 0, X)
            copy(out=windows[name, t][:, 0:X], in_=bank[:])

        def looked_up(name, t, lo, hi):
            return windows[name, t][:].indirect(lookup[name][:, lo * FAN // STRIPE:hi * FAN // STRIPE])

        def gather(name, t, lo, hi):
            found = keep.tile([P, hi - lo, FAN], F32, name="found", tag=FOUND.get((name, t, lo), "found_%s%d_%d" % (name, t, lo)))
            nc.scalar.activation(found[:].rearrange("p x j -> p (x j)"), looked_up(name, t, lo, hi), COPY)
            return found

        def gather_b_onto(from_a, t, lo, hi):
            edges = slots[:, EDGE_SLOTS[t][lo // HALF], lo % HALF:lo % HALF + hi - lo, :]
            nc.vector.tensor_tensor(edges.rearrange("p x j -> p (x j)"), looked_up("b", t, lo, hi),
                                    from_a[:].rearrange("p x j -> p (x j)"), ADD)

        def gather_both(t, lo, hi):
            gather_b_onto(gather("a", t, lo, hi), t, lo, hi)

        def pair_sums(t, lo, hi):
            return slots[:, PAIR_SLOTS[t], :, :].rearrange("p x j -> p (x j)")[:, lo:hi]

        def add_pairs(t, lo, hi):
            low, high = EDGE_SLOTS[t][lo // HALF], EDGE_SLOTS[t][(hi - 1) // HALF]
            width = min(hi - lo, HALF)
            edges = slots[:, low:high + 1:max(high - low, 1), 0:width, :]
            nc.vector.tensor_tensor(pair_sums(t, lo, hi).rearrange("p (h x) -> p h x", x=width),
                                    edges[:, :, :, 0], edges[:, :, :, 1], ADD)

        def add_u(t, lo, hi):
            nc.vector.tensor_tensor(y[:, t, lo:hi], u[t][:, lo:hi], pair_sums(t, lo, hi), ADD)

        def store(first_lane, end_lane, lo, hi):
            nc.sync.dma_start(out=y_rows[:, first_lane:end_lane, lo:hi], in_=y[:, first_lane:end_lane, lo:hi])

        def quantise(lo, hi):
            nc.vector.quantize_mx(out=y_codes[:, lo:hi].bitcast(E4M3), scales=y_scales[:, lo:hi],
                                  in_=y_woven[:, lo:hi, :].rearrange("p x t -> p (x t)"))
            nc.sync.dma_start(out=y_words[:, lo:hi], in_=y_codes[:, lo:hi].bitcast(I32))

        w2 = deal(w2_raw, w2_raw_scales, "w2", 0, 1, nc.vector)
        b_bank = psum.tile([P, X], F32, name="bank", tag="b0")
        product(b_bank[:], w2[0], 0, X)
        w2 = w2 + deal(w2_raw, w2_raw_scales, "w2", 1, LANES, nc.vector)
        open_window("a", 1, "a1", nc.vector, shared, 2 * D + HALF)
        fill("a", w1, 1, "a", nc.vector.tensor_copy)
        nc.vector.tensor_copy(out=windows["b", 0][:, 0:X], in_=b_bank[:])
        second_quarter = shared.tile([P, QUARTER, FAN], F32, name="second_quarter", align_bytes=64, offset=HALF)
        nc.vector.tensor_copy(second_quarter[:].rearrange("p x j -> p (x j)"), looked_up("a", 0, QUARTER, HALF))
        gather_both(0, 0, QUARTER)
        gather_b_onto(second_quarter, 0, QUARTER, HALF)
        gather_both(0, HALF, X)

        w0_words_dealt = keep.tile([P, LANES, P], I32, name="w0_words_dealt", align_bytes=64)
        nc.gpsimd.tensor_copy(out=w0_words_dealt[:], in_=w0_raw[:].rearrange("k (p t) -> k t p", t=LANES))
        w0_scales_dealt = keep.tile([P, LANES, P], U8, name="w0_scales_dealt", align_bytes=64)
        nc.gpsimd.tensor_copy(out=w0_scales_dealt[:], in_=w0_raw_scales[:].rearrange("k (p t) -> k t p", t=LANES))
        w0 = [(w0_words_dealt[:, t, :], w0_scales_dealt[:, t, :]) for t in range(LANES)]
        u = []
        for t in range(LANES):
            u.append(psum.tile([P, X], F32, name="u_bank", tag="u%d" % t if t < LAST else second_part))
            product(u[t][:], w0[t], 0, X)
        fill("b", w2, 1, first_part, nc.vector.tensor_copy)
        add_pairs(0, 0, X)

        u_last = keep.tile([P, X], F32, name="u_last")
        turned = keep.tile([P, LANES, P], F32, name="turned")
        sums = []

        def add_turned(block, found, first, stop):
            for j in range(FAN):
                nc.tensor.matmul(sums[block][:], lhsT=found[:, block * P - first:(block + 1) * P - first, j], rhs=identity[:],
                                 is_transpose=True, start=False, stop=stop and j == FAN - 1)

        def open_with_u(block, tag):
            sums.append(psum.tile([P, P], F32, name="sums", tag=tag))
            nc.tensor.matmul(sums[block][:], lhsT=u_last[:, block * P:(block + 1) * P], rhs=identity[:],
                             is_transpose=True, start=True, stop=False)

        def turn_back(lo, hi, tag, copy):
            bank = psum.tile([P, hi - lo], F32, name="back", tag=tag)
            for block in range(lo // P, hi // P):
                nc.tensor.transpose(bank[:, block * P - lo:(block + 1) * P - lo], turned[:, block, :], identity[:])
            copy(out=y[:, LAST, lo:hi], in_=bank[:])

        found = gather("a", 1, 0, HALF)
        fill("a", w1, 2, "b0", nc.scalar.copy)
        gather_b_onto(found, 1, 0, HALF)
        fill("b", w2, 2, third_part, nc.vector.tensor_copy)
        gather_both(1, HALF, X)
        add_u(0, 0, X)
        store(0, 1, 0, X)
        nc.vector.tensor_copy(out=u_last[:], in_=u[LAST][:])
        add_pairs(1, 0, X)

        gather_both(2, 0, HALF)
        gather_both(2, HALF, X)
        fill("a", w1, 3, "a", nc.scalar.copy)
        fill("b", w2, 3, first_part, nc.scalar.copy)
        add_u(1, 0, X)
        store(1, 2, 0, X)
        add_pairs(2, 0, X)

        for block, tag in enumerate(("a", "b0", "u0", second_part)):
            open_with_u(block, tag)
        early_a = gather("a", LAST, 0, HALF)
        for block in (0, 1):
            add_turned(block, early_a, 0, False)
        early_b = gather("b", LAST, 0, HALF)
        for block in (0, 1):
            add_turned(block, early_b, 0, True)
        late_a = gather("a", LAST, HALF, X)
        for block in (2, 3):
            add_turned(block, late_a, HALF, False)
        for block in (0, 1):
            nc.scalar.copy(out=turned[:, block, :], in_=sums[block][:])
        late_quarters = ((HALF, X - QUARTER), (X - QUARTER, X))
        last_found = keep.tile([P, HALF, FAN], F32, name="last_found", tag=FOUND["b", LAST, 0])
        late_b = [last_found[:, lo - HALF:hi - HALF, :] for lo, hi in late_quarters]
        for (lo, hi), found in zip(late_quarters, late_b):
            nc.scalar.activation(found.rearrange("p x j -> p (x j)"), looked_up("b", LAST, lo, hi), COPY)
        turn_back(0, HALF, third_part, nc.vector.tensor_copy)
        store(LAST, LANES, 0, HALF)
        add_u(LAST - 1, 0, HALF)
        add_u(LAST - 1, HALF, X)
        store(LAST - 1, LAST, 0, X)
        for block, found in zip((2, 3), late_b):
            add_turned(block, found, block * P, True)
            nc.scalar.copy(out=turned[:, block, :], in_=sums[block][:])
        turn_back(HALF, X - QUARTER, first_part, nc.scalar.copy)
        nc.scalar.copy(out=y_woven[:, X - QUARTER:X, 0:LAST].rearrange("p (c i) t -> p c t i", i=4),
                       in_=y[:, 0:LAST, X - QUARTER:X].rearrange("p t (c i) -> p c t i", i=4))
        last_bank = psum.tile([P, QUARTER], F32, name="last_bank", tag="a")
        nc.tensor.transpose(last_bank[:], turned[:, LAST, :], identity[:])
        nc.scalar.copy(out=y_woven[:, X - QUARTER:X, LAST], in_=last_bank[:])
        nc.scalar.copy(out=y[:, LAST, X - QUARTER:X], in_=last_bank[:])
        store(LAST, LANES, HALF, X)
        weave(y_woven, y, 0, HALF, nc.vector.tensor_copy)
        weave(y_woven, y, HALF, X - QUARTER, nc.vector.tensor_copy)
        quantise(0, HALF)
        for lo, hi in late_quarters:
            quantise(lo, hi)
        for q in range(4):
            (nc.sync if q % 2 == 0 else nc.scalar).dma_start(out=out_2[0][4 * q:4 * q + 4, :].bitcast(I32),
                                                             in_=y_scales[32 * q:32 * q + 4, :].bitcast(I32))
